import numpy as np
import ml_dtypes


def mxq(x, axis, fmt="e4m3"):
    dtype, down = {"e4m3": (ml_dtypes.float8_e4m3fn, 7), "e5m2": (ml_dtypes.float8_e5m2, 14)}[fmt]
    v = np.moveaxis(np.asarray(x, np.float32).astype(ml_dtypes.bfloat16).astype(np.float64), axis, -1)
    blocks = v.reshape(v.shape[:-1] + (-1, 32))
    amax = np.abs(blocks).max(-1, keepdims=True)
    byte = np.maximum(np.where(amax > 0, np.frexp(amax)[1] - 1 + 127, 0) - down, 1)
    scale = np.exp2(byte - 127.0)
    codes = (blocks / scale).astype(np.float32).astype(dtype).astype(np.float64)
    return np.moveaxis((codes * scale).reshape(v.shape), -1, axis)


WIDE = False


def mx_kscale(k):
    if not WIDE:
        return np.ones(k)
    levels = np.array([10, -10, 5, -5, 0])
    if k % 512:
        return np.exp2(np.random.permutation(np.resize(levels, k // 32))).repeat(32)
    a = np.empty((k // 512, 16))
    for p in range(k // 512):
        a[p, :8] = np.random.permutation(np.resize(levels, 8))
        for g in range(8):
            far = levels[np.abs(levels - a[p, g]) >= 10]
            a[p, g + 8] = far[np.random.randint(len(far))]
    return np.exp2(a.ravel()).repeat(32)


BF16 = ml_dtypes.bfloat16


def bf(x):
    return np.asarray(x, np.float32).astype(BF16)


def f64(x):
    return np.asarray(x).astype(np.float64)


E2M1 = np.array([0.0, 0.5, 1.0, 1.5, 2.0, 3.0, 4.0, 6.0, -0.0, -0.5, -1.0, -1.5, -2.0, -3.0, -4.0, -6.0])


def pack_weight(w, fmt):
    k, n = w.shape
    w = f64(bf(w)).reshape(k // 32, 32, n)
    amax = np.abs(w).max(1)
    if fmt == "e4m3":
        byte = np.frexp(amax)[1] - 1 + 127 - 7
    else:
        mant, ex = np.frexp(amax / 6.0)
        byte = np.where(mant > 0.5, ex, ex - 1) + 127
    byte = np.clip(np.where(amax > 0, byte, 1), 1, 254)
    scaled = (w * np.exp2(127.0 - byte)[:, None, :]).reshape(k, n).astype(np.float32)
    by_word = np.ascontiguousarray(scaled.reshape(k // 512, 128, 4, n).transpose(0, 1, 3, 2))
    if fmt == "e4m3":
        words = by_word.astype(ml_dtypes.float8_e4m3fn).view(np.uint8)
    else:
        c = by_word.astype(ml_dtypes.float4_e2m1fn).view(np.uint8) & 0xF
        words = c[..., 0::2] | (c[..., 1::2] << 4)
    return np.ascontiguousarray(words), np.ascontiguousarray(byte.astype(np.uint8).reshape(k // 512, 16, n))


def unpack_weight(words, scales, fmt):
    g, p, n, _ = words.shape
    if fmt == "e4m3":
        vals = np.ascontiguousarray(words).view(ml_dtypes.float8_e4m3fn).astype(np.float64)
    else:
        nib = np.empty((g, p, n, 4), np.uint8)
        nib[..., 0::2] = words & 0xF
        nib[..., 1::2] = words >> 4
        vals = E2M1[nib]
    vals = vals * np.repeat(np.exp2(scales.astype(np.float64) - 127.0), 8, axis=1)[..., None]
    return vals.transpose(0, 1, 3, 2).reshape(g * 512, n)
def pack4(w):
    words, scales = pack_weight(w, "e2m1")
    return words.reshape(words.shape[0], 128, -1), scales


def unpack4(words, scales):
    return unpack_weight(words.reshape(words.shape[0], 128, -1, 2), scales, "e2m1")


P, R, S, T, L = 2048, 512, 1024, 1536, 1024


def setup_inputs():
    r, s, t = mx_kscale(R), mx_kscale(T), mx_kscale(S)
    foot = (np.random.standard_normal((R, P)) + 0.2) * r[:, None]
    atom = (np.random.standard_normal((R, S)) + 0.02) / np.sqrt(R) / r[:, None] * t
    foot_words, foot_scales = pack4(foot)
    atom_words, atom_scales = pack4(atom)
    filt = (np.random.standard_normal((S, T)) + 0.05) / np.sqrt(T) / np.sqrt(S) * s / t[:, None]
    occ = np.exp(0.8 * np.random.standard_normal((T, L))) / s[:, None]
    recv = -1.5 - 1.5 * np.random.random_sample(P)
    return {"foot_words": foot_words, "foot_scales": foot_scales,
            "atom_words": atom_words, "atom_scales": atom_scales,
            "filt": bf(filt), "occ": bf(occ), "recv": bf(recv)}


def reference(foot_words, foot_scales, atom_words, atom_scales, filt, occ, recv):
    foot = unpack4(foot_words, foot_scales)
    atom = unpack4(atom_words, atom_scales)
    w = foot.T @ atom
    e = mxq(f64(filt), 1, "e4m3") @ mxq(f64(occ), 0, "e4m3")
    f = w * np.exp(f64(recv))[:, None]
    v = mxq(f, 1, "e4m3") @ mxq(e, 0, "e4m3")
    return np.minimum(v, 1.0)

@@ -1,0 +1,316 @@
+from contextlib import ExitStack
+
+import concourse.mybir as mybir
+from concourse.masks import make_identity
+
+REC, CODES, TEX, RAW, FRM = 2048, 512, 1024, 1536, 1024
+
+FLOPS = 2 * (REC * TEX * CODES + TEX * FRM * RAW + REC * FRM * TEX)
+
+F32 = mybir.dt.float32
+BF16 = mybir.dt.bfloat16
+U32 = mybir.dt.uint32
+I32 = mybir.dt.int32
+U8 = mybir.dt.uint8
+FP8X4 = mybir.dt.float8_e4m3fn_x4
+FP4X4 = mybir.dt.float4_e2m1fn_x4
+EXP = mybir.ActivationFunctionType.Exp
+MULT = mybir.AluOpType.mult
+MIN = mybir.AluOpType.min
+
+P = 128
+BANK = 512
+
+
+def tile_exponential_shadow_visibility_s12_kernel(
+    tc, foot_words, foot_scales, atom_words, atom_scales, filt, occ, recv, out
+):
+    nc = tc.nc
+    n_rt = REC // P
+    n_q = REC // 512
+    n_g = TEX // 512
+    n_c = RAW // 512
+
+    with ExitStack() as ctx:
+        keep = ctx.enter_context(tc.tile_pool(name="keep", bufs=1))
+        work = ctx.enter_context(tc.tile_pool(name="work", bufs=3))
+        outs = ctx.enter_context(tc.tile_pool(name="outs", bufs=6))
+        psum = ctx.enter_context(tc.psum_pool(name="psum", bufs=8))
+        ctx.enter_context(tc.manual_schedule())
+
+        atom_r = keep.tile([P, 2 * TEX], U8, name="atom_r", align_bytes=64)
+        atom_rs = keep.tile([P, TEX], U8, name="atom_rs", align_bytes=64)
+        atom_c = [keep.tile([P, 1024], U8, name=f"atom_c{g}", align_bytes=64) for g in range(n_g)]
+        atom_s = [keep.tile([P, 512], U8, name=f"atom_s{g}", align_bytes=64) for g in range(n_g)]
+        foot_c = keep.tile([P, 2 * REC], U8, name="foot_c", align_bytes=64)
+        foot_s = keep.tile([P, REC], U8, name="foot_s", align_bytes=64)
+        ident = keep.tile([P, P], F32, name="ident")
+        recv_b = keep.tile([P, REC], BF16, name="recv_b")
+        gain = keep.tile([P, REC], F32, name="gain")
+        warm = keep.tile([P, 1], F32, name="warm")
+
+        filt_q = [[keep.tile([P, 512], U32, name=f"filt_q{g}{c}", align_bytes=64) for c in range(n_c)] for g in range(n_g)]
+        filt_s = [[keep.tile([P, 512], U8, name=f"filt_s{g}{c}", align_bytes=64) for c in range(n_c)] for g in range(n_g)]
+        occ_q = [[keep.tile([P, 512], U32, name=f"occ_q{c}{h}", align_bytes=64) for h in range(2)] for c in range(n_c)]
+        occ_s = [[keep.tile([P, 512], U8, name=f"occ_s{c}{h}", align_bytes=64) for h in range(2)] for c in range(n_c)]
+        e_q = [[keep.tile([P, 512], U32, name=f"e_q{g}{h}", align_bytes=64) for h in range(2)] for g in range(n_g)]
+        e_s = [[keep.tile([P, 512], U8, name=f"e_s{g}{h}", align_bytes=64) for h in range(2)] for g in range(n_g)]
+        f_q = [[keep.tile([P, 512], U32, name=f"f_q{q}{g}", align_bytes=64) for g in range(n_g)] for q in range(n_q)]
+        f_s = [[keep.tile([P, 512], U8, name=f"f_s{q}{g}", align_bytes=64) for g in range(n_g)] for q in range(n_q)]
+        filt_x = [[keep.tile([P, 2, RAW], BF16, name=f"filt_x{g}{jp}") for jp in range(2)] for g in range(n_g)]
+        occ_x = [[keep.tile([P, 4, 512], BF16, name=f"occ_x{c}{h}") for h in range(2)] for c in range(n_c)]
+
+        nc.gpsimd.dma_start(out=recv_b[:, 0:512], in_=recv[0:512].partition_broadcast(P))
+        nc.vector.memset(atom_rs[:].bitcast(I32), 0)
+        nc.vector.memset(foot_s[:].bitcast(I32), 0)
+        nc.vector.memset(warm[:], 0.0)
+        nc.sync.dma_start(out=atom_r[:].bitcast(I32), in_=atom_words[0].bitcast(I32))
+        nc.sync.dma_start(out=foot_c[:].bitcast(I32), in_=foot_words[0].bitcast(I32))
+        for q in range(4):
+            nc.scalar.dma_start(
+                out=atom_rs[32 * q : 32 * q + 4, :].bitcast(I32), in_=atom_scales[0][4 * q : 4 * q + 4, :].bitcast(I32)
+            )
+        for q in range(4):
+            (nc.scalar if q < 2 else nc.gpsimd).dma_start(
+                out=foot_s[32 * q : 32 * q + 4, :].bitcast(I32), in_=foot_scales[0][4 * q : 4 * q + 4, :].bitcast(I32)
+            )
+        make_identity(nc, ident[:])
+        nc.scalar.activation(warm[:], warm[:], EXP)
+
+        def load_filt(g, jp):
+            src = filt[512 * g : 512 * (g + 1), :].rearrange("(m j) k -> m j k", j=4)
+            nc.sync.dma_start(out=filt_x[g][jp][:], in_=src[:, 2 * jp : 2 * jp + 2, :])
+
+        def load_occ(c, h):
+            src = occ[512 * c : 512 * (c + 1), :].rearrange("(p j) l -> p j l", j=4)
+            nc.sync.dma_start(out=occ_x[c][h][:], in_=src[:, :, 512 * h : 512 * (h + 1)])
+
+        load_filt(0, 0)
+        load_filt(0, 1)
+        for c in range(n_c):
+            load_occ(c, 0)
+        nc.sync.dma_start(out=recv_b[:, 512:REC], in_=recv[512:REC].partition_broadcast(P))
+        load_filt(1, 0)
+        load_filt(1, 1)
+        for c in range(n_c):
+            load_occ(c, 1)
+
+        def atoms(g):
+            words = atom_r[:, 1024 * g : 1024 * (g + 1)].bitcast(I32)
+            nc.vector.tensor_copy(
+                out=atom_c[g][:].bitcast(I32).rearrange("p (t b w) -> p t b w", t=4, w=2),
+                in_=words.rearrange("p (b t w) -> p t b w", t=4, w=2),
+            )
+            words = atom_rs[:, 512 * g : 512 * (g + 1)].bitcast(I32)
+            nc.vector.tensor_copy(
+                out=atom_s[g][:].bitcast(I32).rearrange("p (t b) -> p t b", t=4),
+                in_=words.rearrange("p (b t) -> p t b", t=4),
+            )
+
+        def gains(q):
+            cols = slice(512 * q, 512 * (q + 1))
+            nc.scalar.activation(gain[:, cols], recv_b[:, cols], EXP)
+
+        w_t = {}
+        f_k = {}
+
+        def w1(q, g, t, engine):
+            cols = slice(512 * q, 512 * (q + 1))
+            if t == 0:
+                w_t[q, g] = work.tile([P, 4, 512], BF16 if engine == "v" else F32, name="w_b" if engine == "v" else "w_f", bufs=2 if engine == "v" else 3)
+            bank = psum.tile([P, BANK], F32, name="bank")
+            nc.tensor.matmul_mx(
+                out=bank[:],
+                lhsT=atom_c[g][:, 256 * t : 256 * (t + 1)].bitcast(FP4X4),
+                lhsT_scale=atom_s[g][:, P * t : P * (t + 1)],
+                rhs=foot_c[:, 1024 * q : 1024 * (q + 1)].bitcast(FP4X4),
+                rhs_scale=foot_s[:, cols],
+                start=True,
+                stop=True,
+            )
+            if engine == "v":
+                nc.vector.tensor_tensor(out=w_t[q, g][:, t, :], in0=bank[:], in1=gain[:, cols], op=MULT)
+            else:
+                nc.scalar.copy(w_t[q, g][:, t, :], bank[:])
+
+        def fi(q, g, engine):
+            f_k[q, g] = work.tile([P, 2048], BF16, name="f_k", bufs=2, align_bytes=64)
+            dst = f_k[q, g][:].rearrange("p (n t) -> p n t", t=4)
+            src = w_t[q, g][:].rearrange("p t n -> p n t")
+            if engine == "v":
+                nc.vector.tensor_copy(out=dst, in_=src)
+            else:
+                mul = gain[:, 512 * q : 512 * (q + 1)].unsqueeze(2).to_broadcast([P, 512, 4])
+                nc.vector.tensor_tensor(out=dst, in0=src, in1=mul, op=MULT)
+
+        def fq(q, g):
+            nc.vector.quantize_mx(out=f_q[q][g][:].bitcast(FP8X4), scales=f_s[q][g][:], in_=f_k[q, g][:])
+
+        filt_k = {}
+
+        def at(g, jp, engine="s"):
+            words = filt_x[g][jp][:].rearrange("p j k -> p (j k)").bitcast(F32)
+            for c in range(n_c):
+                if jp == 0:
+                    filt_k[g, c] = work.tile([P, 2048], BF16, name="filt_k", bufs=4, align_bytes=64)
+                bank = psum.tile([P, BANK], F32, name="bank")
+                for j in range(2):
+                    for u in range(2):
+                        w0 = 768 * j + 256 * c + u
+                        b = 2 * j + u
+                        nc.tensor.transpose(bank[:, P * b : P * (b + 1)], words[:, w0 : 768 * j + 256 * (c + 1) : 2], ident[:])
+                dst = filt_k[g, c][:].bitcast(F32).rearrange("p (t b x) -> p t b x", t=4, x=8)[:, :, :, 4 * jp : 4 * jp + 4]
+                src = bank[:].rearrange("p (x b t) -> p t b x", t=4, x=4)
+                if engine == "v":
+                    nc.vector.tensor_copy(out=dst, in_=src)
+                else:
+                    nc.scalar.copy(dst, src)
+
+        def aq(g, c):
+            nc.vector.quantize_mx(out=filt_q[g][c][:].bitcast(FP8X4), scales=filt_s[g][c][:], in_=filt_k[g, c][:])
+
+        occ_k = {}
+
+        def bi(c, h, engine="v"):
+            occ_k[c, h] = work.tile([P, 2048], BF16, name="occ_k", bufs=3, align_bytes=64)
+            dst = occ_k[c, h][:].rearrange("p (l j) -> p l j", j=4)
+            src = occ_x[c][h][:].rearrange("p j l -> p l j")
+            if engine == "v":
+                nc.vector.tensor_copy(out=dst, in_=src)
+            else:
+                nc.scalar.copy(dst, src)
+
+        def bq(c, h):
+            nc.vector.quantize_mx(out=occ_q[c][h][:].bitcast(FP8X4), scales=occ_s[c][h][:], in_=occ_k[c, h][:])
+
+        e_k = {}
+
+        def s2(g, h, i, engine="s"):
+            if i == 0:
+                e_k[g, h] = work.tile([P, 2048], BF16, name="e_k", bufs=3, align_bytes=64)
+            bank = psum.tile([P, BANK], F32, name="bank")
+            for t in range(4):
+                for c in range(n_c):
+                    nc.tensor.matmul_mx(
+                        out=bank[:, P * t : P * (t + 1)],
+                        lhsT=filt_q[g][c][:, P * t : P * (t + 1)].bitcast(FP8X4),
+                        lhsT_scale=filt_s[g][c][:, P * t : P * (t + 1)],
+                        rhs=occ_q[c][h][:, P * i : P * (i + 1)].bitcast(FP8X4),
+                        rhs_scale=occ_s[c][h][:, P * i : P * (i + 1)],
+                        start=(c == 0),
+                        stop=(c == n_c - 1),
+                    )
+            dst = e_k[g, h][:, 512 * i : 512 * (i + 1)].rearrange("p (n t) -> p n t", t=4)
+            src = bank[:].rearrange("p (t n) -> p n t", t=4)
+            if engine == "v":
+                nc.vector.tensor_copy(out=dst, in_=src)
+            else:
+                nc.scalar.copy(dst, src)
+
+        def eq(g, h):
+            nc.vector.quantize_mx(out=e_q[g][h][:].bitcast(FP8X4), scales=e_s[g][h][:], in_=e_k[g, h][:])
+
+        out_t = {}
+
+        def s3(rt, h, engine):
+            q, i = rt // 4, rt % 4
+            if rt not in out_t:
+                out_t[rt] = outs.tile([P, FRM], F32, name="out_t")
+            bank = psum.tile([P, BANK], F32, name="bank")
+            for g in range(n_g):
+                nc.tensor.matmul_mx(
+                    out=bank[:],
+                    lhsT=f_q[q][g][:, P * i : P * (i + 1)].bitcast(FP8X4),
+                    lhsT_scale=f_s[q][g][:, P * i : P * (i + 1)],
+                    rhs=e_q[g][h][:].bitcast(FP8X4),
+                    rhs_scale=e_s[g][h][:],
+                    start=(g == 0),
+                    stop=(g == n_g - 1),
+                )
+            dst = out_t[rt][:, 512 * h : 512 * (h + 1)]
+            if engine == "v":
+                nc.vector.tensor_scalar_min(dst, bank[:], 1.0)
+            else:
+                nc.scalar.copy(dst, bank[:])
+                nc.gpsimd.tensor_scalar(dst, dst, 1.0, 1.0, MULT, MIN)
+            nc.sync.dma_start(out=out[P * rt : P * (rt + 1), 512 * h : 512 * (h + 1)], in_=dst)
+
+        atoms(0)
+        atoms(1)
+        gains(0)
+        for t in range(4):
+            w1(0, 0, t, "v")
+        for t in range(4):
+            w1(0, 1, t, "v")
+        at(0, 0)
+        at(0, 1)
+        fi(0, 0, "v")
+        bi(0, 0, "s")
+        for c in range(n_c):
+            aq(0, c)
+        fq(0, 0)
+        bi(1, 0)
+        for t in range(4):
+            w1(1, 0, t, "s")
+        bi(2, 0)
+        for c in range(n_c):
+            bq(c, 0)
+        at(1, 0)
+        at(1, 1)
+        fi(0, 1, "v")
+        bi(0, 1)
+        for i in range(4):
+            s2(0, 0, i)
+        gains(1)
+        gains(2)
+        for t in range(4):
+            w1(1, 1, t, "s")
+        for c in range(n_c):
+            aq(1, c)
+        fq(0, 1)
+        bi(1, 1)
+        bi(2, 1)
+        eq(0, 0)
+        for c in range(n_c):
+            bq(c, 1)
+        gains(3)
+        for t in range(4):
+            w1(2, 0, t, "s")
+        for i in range(4):
+            s2(1, 0, i)
+        for t in range(4):
+            w1(2, 1, t, "s")
+        fi(1, 0, "s")
+        eq(1, 0)
+        fi(1, 1, "s")
+        for i in range(4):
+            s2(0, 1, i)
+        fq(1, 0)
+        for i in range(4):
+            s2(1, 1, i)
+        eq(0, 1)
+        fq(1, 1)
+        fi(2, 0, "s")
+        for rt in range(4):
+            s3(rt, 0, "s")
+        eq(1, 1)
+        for t in range(4):
+            w1(3, 0, t, "s")
+        fi(2, 1, "s")
+        fq(2, 0)
+        for rt in range(4):
+            s3(rt, 1, "sv"[rt % 2])
+        for t in range(4):
+            w1(3, 1, t, "s")
+        fq(2, 1)
+        fi(3, 0, "s")
+        for rt in range(4, 8):
+            s3(rt, 0, "s")
+        fi(3, 1, "s")
+        fq(3, 0)
+        for rt in range(4, 8):
+            s3(rt, 1, "sv"[rt % 2])
+        fq(3, 1)
+        for rt in range(8, 16):
+            s3(rt, 0, "s")
+            s3(rt, 1, "v")

@@ -14,12 +14,22 @@ I32 = mybir.dt.int32
 U8 = mybir.dt.uint8
 FP8X4 = mybir.dt.float8_e4m3fn_x4
 FP4X4 = mybir.dt.float4_e2m1fn_x4
+COPY = mybir.ActivationFunctionType.Copy
 EXP = mybir.ActivationFunctionType.Exp
-MULT = mybir.AluOpType.mult
-MIN = mybir.AluOpType.min
 
 P = 128
 BANK = 512
+
+LOADS = ["f00","f01","o00","o10","o20","f10","f11","o01","o11","o21"]
+T_ORDER = """
+gt F.1.1 F.0.0 F.4.0 F.2.1 F.4.1 F.3.1 F.6.1 F.5.1 F.0.1 F.2.0 F.1.0 F.9.0 AT.0.0.2 AT.0.0.1 AT.0.1.1 AT.0.1.2 F.3.0 T.1 T.2 AT.0.0.0 AT.0.1.0 F.7.0 T.0 AT.1.0.0 AT.1.0.1 T.3 AT.1.0.2 AT.1.1.1 AT.1.1.2 AT.1.1.0 T.4 F.5.0 F.6.0 F.7.1 F.10.1 F.8.0 S2.0.0.1 S2.0.0.0 F.9.1 F.8.1 S2.0.0.3 S2.0.0.2 S2.1.0.1 F.13.0 S2.1.0.3 S2.1.0.0 S2.1.0.2 F.12.1 F.11.0 T.5 S2.1.1.3 S2.0.1.0 F.11.1 S2.0.1.3 S2.0.1.1 S2.0.1.2 S2.1.1.0 F.10.0 T.6 T.8 T.7 T.9 F.13.1 S2.1.1.2 F.14.0 F.12.0 S2.1.1.1 S3.9.0 S3.3.0 S3.2.0 T.10 T.11 S3.1.0 S3.0.0 S3.2.1 F.15.0 S3.5.1 F.14.1 F.15.1 S3.9.1 S3.0.1 S3.1.1 S3.6.1 S3.3.1 T.12 T.13 S3.11.1 S3.4.1 S3.10.1 S3.8.0 S3.5.0 S3.6.0 T.15 T.14 S3.13.1 S3.7.1 S3.13.0 S3.10.0 S3.12.1 S3.11.0 S3.14.0 S3.15.0 S3.14.1 S3.4.0 S3.7.0 S3.15.1 S3.12.0 S3.8.1
+"""
+V_ORDER = """
+D.1.1 D.4.0 D.3.1 D.6.1 D.0.1 D.9.0 B.0.0 B.1.0 W.2 B.2.0 AQ.0.1 BQ.2.0 BQ.0.0 A.1.0.1 AQ.0.0 AQ.0.2 BQ.1.0 AQ.1.0 D.7.1 AQ.1.1 C.0.0.1 AQ.1.2 D.8.1 B.2.1 B.0.1 BQ.2.1 BQ.1.1 BQ.0.1 W.5 FQ.0 EQ.1.0 C.0.1.1 FQ.2 C.1.1.0 W.6 EQ.0.1 D.10.0 FQ.4 EQ.0.0 FQ.1 O.9.0 O.3.0 EQ.1.1 FQ.3 O.2.0 O.0.0 O.1.0 FQ.5 O.2.1 O.5.1 O.0.1 O.9.1 O.1.1 O.6.1 O.3.1 O.11.1 FQ.6 O.4.1 O.8.0 O.5.0 O.10.1 O.6.0 O.13.1 O.7.1 FQ.7 O.13.0 O.12.1 O.11.0 O.10.0 O.14.0 O.15.0 O.4.0 O.14.1 O.12.0 O.8.1 O.7.0 O.15.1
+"""
+S_ORDER = """
+gs D.0.0 D.2.1 D.4.1 D.5.1 D.2.0 A.0.0.2 D.1.0 A.0.1.1 A.0.0.1 D.3.0 W.1 A.0.1.2 A.0.0.0 D.7.0 A.1.0.0 A.0.1.0 W.0 W.3 A.1.1.1 A.1.0.2 A.1.1.2 A.1.1.0 D.5.0 W.4 D.6.0 D.10.1 D.8.0 C.0.0.0 B.1.1 D.9.1 C.0.0.3 C.0.0.2 C.1.0.1 C.1.0.3 D.13.0 C.1.0.2 C.1.0.0 C.1.1.3 C.0.1.0 D.12.1 D.11.0 C.0.1.3 C.0.1.2 D.11.1 W.8 W.9 D.13.1 W.7 D.14.0 D.12.0 C.1.1.1 C.1.1.2 W.10 W.11 D.14.1 D.15.0 D.15.1 W.12 W.13 W.14 W.15
+"""
 
 
 def tile_exponential_shadow_visibility_s12_kernel(
@@ -27,48 +37,47 @@ def tile_exponential_shadow_visibility_s12_kernel(
 ):
     nc = tc.nc
     n_rt = REC // P
-    n_q = REC // 512
     n_g = TEX // 512
     n_c = RAW // 512
 
     with ExitStack() as ctx:
         keep = ctx.enter_context(tc.tile_pool(name="keep", bufs=1))
         work = ctx.enter_context(tc.tile_pool(name="work", bufs=3))
-        outs = ctx.enter_context(tc.tile_pool(name="outs", bufs=6))
+        outs = ctx.enter_context(tc.tile_pool(name="outs", bufs=10))
         psum = ctx.enter_context(tc.psum_pool(name="psum", bufs=8))
         ctx.enter_context(tc.manual_schedule())
 
-        atom_r = keep.tile([P, 2 * TEX], U8, name="atom_r", align_bytes=64)
-        atom_rs = keep.tile([P, TEX], U8, name="atom_rs", align_bytes=64)
-        atom_c = [keep.tile([P, 1024], U8, name=f"atom_c{g}", align_bytes=64) for g in range(n_g)]
-        atom_s = [keep.tile([P, 512], U8, name=f"atom_s{g}", align_bytes=64) for g in range(n_g)]
+        atom_c = keep.tile([P, 2 * TEX], U8, name="atom_c", align_bytes=64)
+        atom_s = keep.tile([P, TEX], U8, name="atom_s", align_bytes=64)
         foot_c = keep.tile([P, 2 * REC], U8, name="foot_c", align_bytes=64)
         foot_s = keep.tile([P, REC], U8, name="foot_s", align_bytes=64)
         ident = keep.tile([P, P], F32, name="ident")
-        recv_b = keep.tile([P, REC], BF16, name="recv_b")
-        gain = keep.tile([P, REC], F32, name="gain")
+        rows16 = keep.tile([P, P], BF16, name="rows16")
+        rows32 = keep.tile([P, P], F32, name="rows32")
+        gain = keep.tile([P, n_rt], F32, name="gain")
         warm = keep.tile([P, 1], F32, name="warm")
-
         filt_q = [[keep.tile([P, 512], U32, name=f"filt_q{g}{c}", align_bytes=64) for c in range(n_c)] for g in range(n_g)]
         filt_s = [[keep.tile([P, 512], U8, name=f"filt_s{g}{c}", align_bytes=64) for c in range(n_c)] for g in range(n_g)]
         occ_q = [[keep.tile([P, 512], U32, name=f"occ_q{c}{h}", align_bytes=64) for h in range(2)] for c in range(n_c)]
         occ_s = [[keep.tile([P, 512], U8, name=f"occ_s{c}{h}", align_bytes=64) for h in range(2)] for c in range(n_c)]
         e_q = [[keep.tile([P, 512], U32, name=f"e_q{g}{h}", align_bytes=64) for h in range(2)] for g in range(n_g)]
         e_s = [[keep.tile([P, 512], U8, name=f"e_s{g}{h}", align_bytes=64) for h in range(2)] for g in range(n_g)]
-        f_q = [[keep.tile([P, 512], U32, name=f"f_q{q}{g}", align_bytes=64) for g in range(n_g)] for q in range(n_q)]
-        f_s = [[keep.tile([P, 512], U8, name=f"f_s{q}{g}", align_bytes=64) for g in range(n_g)] for q in range(n_q)]
+        f_q = [keep.tile([P, 512], U32, name=f"f_q{k}", align_bytes=64) for k in range(n_rt // 2)]
+        f_s = [keep.tile([P, 512], U8, name=f"f_s{k}", align_bytes=64) for k in range(n_rt // 2)]
         filt_x = [[keep.tile([P, 2, RAW], BF16, name=f"filt_x{g}{jp}") for jp in range(2)] for g in range(n_g)]
         occ_x = [[keep.tile([P, 4, 512], BF16, name=f"occ_x{c}{h}") for h in range(2)] for c in range(n_c)]
+        occ_k = [[None, None] for c in range(n_c)]
 
-        nc.gpsimd.dma_start(out=recv_b[:, 0:512], in_=recv[0:512].partition_broadcast(P))
-        nc.vector.memset(atom_rs[:].bitcast(I32), 0)
+        nc.vector.memset(rows16[:], 0.0)
+        nc.vector.memset(atom_s[:].bitcast(I32), 0)
         nc.vector.memset(foot_s[:].bitcast(I32), 0)
         nc.vector.memset(warm[:], 0.0)
-        nc.sync.dma_start(out=atom_r[:].bitcast(I32), in_=atom_words[0].bitcast(I32))
+        nc.sync.dma_start(out=atom_c[:].bitcast(I32), in_=atom_words[0].bitcast(I32))
         nc.sync.dma_start(out=foot_c[:].bitcast(I32), in_=foot_words[0].bitcast(I32))
+        nc.gpsimd.dma_start(out=rows16[0:n_rt, :], in_=recv.rearrange("(c n) -> c n", n=P))
         for q in range(4):
             nc.scalar.dma_start(
-                out=atom_rs[32 * q : 32 * q + 4, :].bitcast(I32), in_=atom_scales[0][4 * q : 4 * q + 4, :].bitcast(I32)
+                out=atom_s[32 * q : 32 * q + 4, :].bitcast(I32), in_=atom_scales[0][4 * q : 4 * q + 4, :].bitcast(I32)
             )
         for q in range(4):
             (nc.scalar if q < 2 else nc.gpsimd).dma_start(
@@ -85,110 +94,119 @@ def tile_exponential_shadow_visibility_s12_kernel(
             src = occ[512 * c : 512 * (c + 1), :].rearrange("(p j) l -> p j l", j=4)
             nc.sync.dma_start(out=occ_x[c][h][:], in_=src[:, :, 512 * h : 512 * (h + 1)])
 
-        load_filt(0, 0)
-        load_filt(0, 1)
-        for c in range(n_c):
-            load_occ(c, 0)
-        nc.sync.dma_start(out=recv_b[:, 512:REC], in_=recv[512:REC].partition_broadcast(P))
-        load_filt(1, 0)
-        load_filt(1, 1)
-        for c in range(n_c):
-            load_occ(c, 1)
+        for step in LOADS:
+            if step[0] == "f":
+                load_filt(int(step[1]), int(step[2]))
+            else:
+                load_occ(int(step[1]), int(step[2]))
 
-        def atoms(g):
-            words = atom_r[:, 1024 * g : 1024 * (g + 1)].bitcast(I32)
-            nc.vector.tensor_copy(
-                out=atom_c[g][:].bitcast(I32).rearrange("p (t b w) -> p t b w", t=4, w=2),
-                in_=words.rearrange("p (b t w) -> p t b w", t=4, w=2),
-            )
-            words = atom_rs[:, 512 * g : 512 * (g + 1)].bitcast(I32)
-            nc.vector.tensor_copy(
-                out=atom_s[g][:].bitcast(I32).rearrange("p (t b) -> p t b", t=4),
-                in_=words.rearrange("p (b t) -> p t b", t=4),
-            )
+        nc.vector.tensor_copy(out=rows32[:], in_=rows16[:])
 
-        def gains(q):
-            cols = slice(512 * q, 512 * (q + 1))
-            nc.scalar.activation(gain[:, cols], recv_b[:, cols], EXP)
+        ops = {}
 
-        w_t = {}
+        def op(name, needs, fn):
+            ops[name] = (needs, fn)
+
+        banks = {}
+
+        def new_bank(key):
+            bank = psum.tile([P, BANK], F32, name="bank")
+            banks[key] = bank
+            return bank
+
+        def gain_t():
+            nc.tensor.transpose(new_bank("gain")[:, 0:P], rows32[:], ident[:])
+
+        def gain_s():
+            nc.scalar.activation(gain[:], banks["gain"][:, 0:n_rt], EXP)
+
+        op("gt", [], gain_t)
+        op("gs", ["gt"], gain_s)
+
+        f_nat = {}
         f_k = {}
 
-        def w1(q, g, t, engine):
-            cols = slice(512 * q, 512 * (q + 1))
-            if t == 0:
-                w_t[q, g] = work.tile([P, 4, 512], BF16 if engine == "v" else F32, name="w_b" if engine == "v" else "w_f", bufs=2 if engine == "v" else 3)
-            bank = psum.tile([P, BANK], F32, name="bank")
+        def f1(rt, g):
             nc.tensor.matmul_mx(
-                out=bank[:],
-                lhsT=atom_c[g][:, 256 * t : 256 * (t + 1)].bitcast(FP4X4),
-                lhsT_scale=atom_s[g][:, P * t : P * (t + 1)],
-                rhs=foot_c[:, 1024 * q : 1024 * (q + 1)].bitcast(FP4X4),
-                rhs_scale=foot_s[:, cols],
+                out=new_bank(("f", rt, g))[:],
+                lhsT=foot_c[:, 256 * rt : 256 * (rt + 1)].bitcast(FP4X4),
+                lhsT_scale=foot_s[:, P * rt : P * (rt + 1)],
+                rhs=atom_c[:, 1024 * g : 1024 * (g + 1)].bitcast(FP4X4),
+                rhs_scale=atom_s[:, 512 * g : 512 * (g + 1)],
                 start=True,
                 stop=True,
             )
-            if engine == "v":
-                nc.vector.tensor_tensor(out=w_t[q, g][:, t, :], in0=bank[:], in1=gain[:, cols], op=MULT)
-            else:
-                nc.scalar.copy(w_t[q, g][:, t, :], bank[:])
 
-        def fi(q, g, engine):
-            f_k[q, g] = work.tile([P, 2048], BF16, name="f_k", bufs=2, align_bytes=64)
-            dst = f_k[q, g][:].rearrange("p (n t) -> p n t", t=4)
-            src = w_t[q, g][:].rearrange("p t n -> p n t")
-            if engine == "v":
+        def fd(rt, g, engine):
+            if rt not in f_nat:
+                f_nat[rt] = work.tile([P, TEX], BF16, name="nat", bufs=8)
+            dst = f_nat[rt][:, 512 * g : 512 * (g + 1)].rearrange("p (u w e) -> p u w e", u=2, e=2)
+            src = banks["f", rt, g][:].rearrange("p (w u e) -> p u w e", u=2, e=2)
+            if engine == "V":
+                nc.vector.tensor_scalar_mul(dst, src, gain[:, rt : rt + 1])
+            else:
+                nc.scalar.activation(dst, src, COPY, scale=gain[:, rt : rt + 1])
+
+        def ft(rt):
+            words = f_nat[rt][:].bitcast(F32)
+            bank = new_bank(("t", rt))
+            for b in range(4):
+                nc.tensor.transpose(bank[:, P * b : P * (b + 1)], words[:, P * b : P * (b + 1)], ident[:])
+
+        def fw(rt, engine):
+            k, i = rt // 2, rt % 2
+            if k not in f_k:
+                f_k[k] = work.tile([P, 2048], BF16, name="f_kt", bufs=4, align_bytes=64)
+            dst = f_k[k][:, 1024 * i : 1024 * (i + 1)].bitcast(F32).rearrange("p (g r u) -> p g r u", g=2, u=2)
+            src = banks["t", rt][:].rearrange("p (g u r) -> p g r u", g=2, u=2)
+            if engine == "V":
                 nc.vector.tensor_copy(out=dst, in_=src)
             else:
-                mul = gain[:, 512 * q : 512 * (q + 1)].unsqueeze(2).to_broadcast([P, 512, 4])
-                nc.vector.tensor_tensor(out=dst, in0=src, in1=mul, op=MULT)
+                nc.scalar.copy(dst, src)
 
-        def fq(q, g):
-            nc.vector.quantize_mx(out=f_q[q][g][:].bitcast(FP8X4), scales=f_s[q][g][:], in_=f_k[q, g][:])
+        def fq(k):
+            nc.vector.quantize_mx(out=f_q[k][:].bitcast(FP8X4), scales=f_s[k][:], in_=f_k[k][:])
 
         filt_k = {}
 
-        def at(g, jp, engine="s"):
+        def at(g, jp, c):
             words = filt_x[g][jp][:].rearrange("p j k -> p (j k)").bitcast(F32)
-            for c in range(n_c):
-                if jp == 0:
-                    filt_k[g, c] = work.tile([P, 2048], BF16, name="filt_k", bufs=4, align_bytes=64)
-                bank = psum.tile([P, BANK], F32, name="bank")
-                for j in range(2):
-                    for u in range(2):
-                        w0 = 768 * j + 256 * c + u
-                        b = 2 * j + u
-                        nc.tensor.transpose(bank[:, P * b : P * (b + 1)], words[:, w0 : 768 * j + 256 * (c + 1) : 2], ident[:])
-                dst = filt_k[g, c][:].bitcast(F32).rearrange("p (t b x) -> p t b x", t=4, x=8)[:, :, :, 4 * jp : 4 * jp + 4]
-                src = bank[:].rearrange("p (x b t) -> p t b x", t=4, x=4)
-                if engine == "v":
-                    nc.vector.tensor_copy(out=dst, in_=src)
-                else:
-                    nc.scalar.copy(dst, src)
+            bank = new_bank(("a", g, jp, c))
+            for j in range(2):
+                for u in range(2):
+                    w0 = 768 * j + 256 * c
+                    b = 2 * j + u
+                    nc.tensor.transpose(bank[:, P * b : P * (b + 1)], words[:, w0 + u : w0 + 256 : 2], ident[:])
+
+        def ac(g, jp, c, engine):
+            if (g, c) not in filt_k:
+                filt_k[g, c] = work.tile([P, 2048], BF16, name="filt_k", bufs=6, align_bytes=64)
+            dst = filt_k[g, c][:, 1024 * jp : 1024 * (jp + 1)].bitcast(F32).rearrange("p (j m u) -> p j m u", j=2, u=2)
+            src = banks["a", g, jp, c][:].rearrange("p (j u m) -> p j m u", j=2, u=2)
+            if engine == "V":
+                nc.vector.tensor_copy(out=dst, in_=src)
+            else:
+                nc.scalar.copy(dst, src)
 
         def aq(g, c):
             nc.vector.quantize_mx(out=filt_q[g][c][:].bitcast(FP8X4), scales=filt_s[g][c][:], in_=filt_k[g, c][:])
 
-        occ_k = {}
-
-        def bi(c, h, engine="v"):
-            occ_k[c, h] = work.tile([P, 2048], BF16, name="occ_k", bufs=3, align_bytes=64)
-            dst = occ_k[c, h][:].rearrange("p (l j) -> p l j", j=4)
+        def bi(c, h, engine):
+            occ_k[c][h] = work.tile([P, 2048], BF16, name="occ_kt", bufs=6, align_bytes=64)
+            dst = occ_k[c][h][:].rearrange("p (l j) -> p l j", j=4)
             src = occ_x[c][h][:].rearrange("p j l -> p l j")
-            if engine == "v":
+            if engine == "V":
                 nc.vector.tensor_copy(out=dst, in_=src)
             else:
                 nc.scalar.copy(dst, src)
 
         def bq(c, h):
-            nc.vector.quantize_mx(out=occ_q[c][h][:].bitcast(FP8X4), scales=occ_s[c][h][:], in_=occ_k[c, h][:])
+            nc.vector.quantize_mx(out=occ_q[c][h][:].bitcast(FP8X4), scales=occ_s[c][h][:], in_=occ_k[c][h][:])
 
         e_k = {}
 
-        def s2(g, h, i, engine="s"):
-            if i == 0:
-                e_k[g, h] = work.tile([P, 2048], BF16, name="e_k", bufs=3, align_bytes=64)
-            bank = psum.tile([P, BANK], F32, name="bank")
+        def s2(g, h, i):
+            bank = new_bank(("s", g, h, i))
             for t in range(4):
                 for c in range(n_c):
                     nc.tensor.matmul_mx(
@@ -200,9 +218,13 @@ def tile_exponential_shadow_visibility_s12_kernel(
                         start=(c == 0),
                         stop=(c == n_c - 1),
                     )
+
+        def ec(g, h, i, engine):
+            if (g, h) not in e_k:
+                e_k[g, h] = work.tile([P, 2048], BF16, name="e_kt", bufs=4, align_bytes=64)
             dst = e_k[g, h][:, 512 * i : 512 * (i + 1)].rearrange("p (n t) -> p n t", t=4)
-            src = bank[:].rearrange("p (t n) -> p n t", t=4)
-            if engine == "v":
+            src = banks["s", g, h, i][:].rearrange("p (t n) -> p n t", t=4)
+            if engine == "V":
                 nc.vector.tensor_copy(out=dst, in_=src)
             else:
                 nc.scalar.copy(dst, src)
@@ -212,105 +234,93 @@ def tile_exponential_shadow_visibility_s12_kernel(
 
         out_t = {}
 
-        def s3(rt, h, engine):
-            q, i = rt // 4, rt % 4
-            if rt not in out_t:
-                out_t[rt] = outs.tile([P, FRM], F32, name="out_t")
-            bank = psum.tile([P, BANK], F32, name="bank")
+        def s3(rt, h):
+            k, i = rt // 2, rt % 2
+            bank = new_bank(("o", rt, h))
             for g in range(n_g):
+                cols = slice(P * (2 * i + g), P * (2 * i + g + 1))
                 nc.tensor.matmul_mx(
                     out=bank[:],
-                    lhsT=f_q[q][g][:, P * i : P * (i + 1)].bitcast(FP8X4),
-                    lhsT_scale=f_s[q][g][:, P * i : P * (i + 1)],
+                    lhsT=f_q[k][:, cols].bitcast(FP8X4),
+                    lhsT_scale=f_s[k][:, cols],
                     rhs=e_q[g][h][:].bitcast(FP8X4),
                     rhs_scale=e_s[g][h][:],
                     start=(g == 0),
                     stop=(g == n_g - 1),
                 )
-            dst = out_t[rt][:, 512 * h : 512 * (h + 1)]
-            if engine == "v":
-                nc.vector.tensor_scalar_min(dst, bank[:], 1.0)
+
+        def od(rt, h, engine):
+            out_t[rt, h] = outs.tile([P, 512], F32, name="out_t")
+            dst = out_t[rt, h][:]
+            if engine == "V":
+                nc.vector.tensor_scalar_min(dst, banks["o", rt, h][:], 1.0)
+                nc.sync.dma_start(out=out[P * rt : P * (rt + 1), 512 * h : 512 * (h + 1)], in_=dst)
             else:
-                nc.scalar.copy(dst, bank[:])
-                nc.gpsimd.tensor_scalar(dst, dst, 1.0, 1.0, MULT, MIN)
+                nc.scalar.copy(dst, banks["o", rt, h][:])
+
+        def om(rt, h):
+            dst = out_t[rt, h][:]
+            nc.vector.tensor_scalar_min(dst, dst, 1.0)
             nc.sync.dma_start(out=out[P * rt : P * (rt + 1), 512 * h : 512 * (h + 1)], in_=dst)
 
-        atoms(0)
-        atoms(1)
-        gains(0)
-        for t in range(4):
-            w1(0, 0, t, "v")
-        for t in range(4):
-            w1(0, 1, t, "v")
-        at(0, 0)
-        at(0, 1)
-        fi(0, 0, "v")
-        bi(0, 0, "s")
-        for c in range(n_c):
-            aq(0, c)
-        fq(0, 0)
-        bi(1, 0)
-        for t in range(4):
-            w1(1, 0, t, "s")
-        bi(2, 0)
-        for c in range(n_c):
-            bq(c, 0)
-        at(1, 0)
-        at(1, 1)
-        fi(0, 1, "v")
-        bi(0, 1)
-        for i in range(4):
-            s2(0, 0, i)
-        gains(1)
-        gains(2)
-        for t in range(4):
-            w1(1, 1, t, "s")
-        for c in range(n_c):
-            aq(1, c)
-        fq(0, 1)
-        bi(1, 1)
-        bi(2, 1)
-        eq(0, 0)
-        for c in range(n_c):
-            bq(c, 1)
-        gains(3)
-        for t in range(4):
-            w1(2, 0, t, "s")
-        for i in range(4):
-            s2(1, 0, i)
-        for t in range(4):
-            w1(2, 1, t, "s")
-        fi(1, 0, "s")
-        eq(1, 0)
-        fi(1, 1, "s")
-        for i in range(4):
-            s2(0, 1, i)
-        fq(1, 0)
-        for i in range(4):
-            s2(1, 1, i)
-        eq(0, 1)
-        fq(1, 1)
-        fi(2, 0, "s")
-        for rt in range(4):
-            s3(rt, 0, "s")
-        eq(1, 1)
-        for t in range(4):
-            w1(3, 0, t, "s")
-        fi(2, 1, "s")
-        fq(2, 0)
-        for rt in range(4):
-            s3(rt, 1, "sv"[rt % 2])
-        for t in range(4):
-            w1(3, 1, t, "s")
-        fq(2, 1)
-        fi(3, 0, "s")
-        for rt in range(4, 8):
-            s3(rt, 0, "s")
-        fi(3, 1, "s")
-        fq(3, 0)
-        for rt in range(4, 8):
-            s3(rt, 1, "sv"[rt % 2])
-        fq(3, 1)
-        for rt in range(8, 16):
-            s3(rt, 0, "s")
-            s3(rt, 1, "v")
+        def run(token):
+            a = token.split(".")
+            n = [int(x) for x in a[1:] if x not in ("V", "S")]
+            e = a[len(a) - 1]
+            k = a[0]
+            if k == "gt":
+                return [], gain_t
+            if k == "gs":
+                return ["gt"], gain_s
+            if k == "F":
+                return [], lambda: f1(*n)
+            if k == "D":
+                return ["gs", "F.%d.%d" % (n[0], n[1])], lambda: fd(n[0], n[1], e)
+            if k == "T":
+                return ["D.%d.0" % n[0], "D.%d.1" % n[0]], lambda: ft(*n)
+            if k == "W":
+                return ["T.%d" % n[0]], lambda: fw(n[0], e)
+            if k == "FQ":
+                return ["W.%d" % (2 * n[0]), "W.%d" % (2 * n[0] + 1)], lambda: fq(*n)
+            if k == "AT":
+                return [], lambda: at(*n)
+            if k == "A":
+                return ["AT.%d.%d.%d" % (n[0], n[1], n[2])], lambda: ac(n[0], n[1], n[2], e)
+            if k == "AQ":
+                return ["A.%d.%d.%d" % (n[0], jp, n[1]) for jp in range(2)], lambda: aq(*n)
+            if k == "B":
+                return [], lambda: bi(n[0], n[1], e)
+            if k == "BQ":
+                return ["B.%d.%d" % (n[0], n[1])], lambda: bq(*n)
+            if k == "S2":
+                return ["AQ.%d.%d" % (n[0], c) for c in range(3)] + ["BQ.%d.%d" % (c, n[1]) for c in range(3)], lambda: s2(*n)
+            if k == "C":
+                return ["S2.%d.%d.%d" % (n[0], n[1], n[2])], lambda: ec(n[0], n[1], n[2], e)
+            if k == "EQ":
+                return ["C.%d.%d.%d" % (n[0], n[1], i) for i in range(4)], lambda: eq(*n)
+            if k == "S3":
+                return ["FQ.%d" % (n[0] // 2)] + ["EQ.%d.%d" % (g, n[1]) for g in range(2)], lambda: s3(*n)
+            if k == "O":
+                return ["S3.%d.%d" % (n[0], n[1])], lambda: od(n[0], n[1], e)
+            if k == "M":
+                return ["O.%d.%d" % (n[0], n[1])], lambda: om(*n)
+            raise ValueError(token)
+
+        queues = [T_ORDER.split(), V_ORDER.split(), S_ORDER.split()]
+        names = ["", ".V", ".S"]
+        done = set()
+        at_q = [0, 0, 0]
+        total = sum([len(q) for q in queues])
+        while len(done) < total:
+            before = len(done)
+            for j in range(3):
+                while at_q[j] < len(queues[j]):
+                    token = queues[j][at_q[j]]
+                    needs, fn = run(token + names[j])
+                    if not all([x in done for x in needs]):
+                        break
+                    fn()
+                    done.add(token)
+                    at_q[j] += 1
+            if len(done) == before:
+                raise ValueError([q[i] for q, i in zip(queues, at_q) if i < len(q)])

@@ -19,16 +19,33 @@ EXP = mybir.ActivationFunctionType.Exp
 
 P = 128
 BANK = 512
+TPQ = (2, 3,)
+SPLIT_D = True
 
-LOADS = ["f00","f01","o00","o10","o20","f10","f11","o01","o11","o21"]
+LOADS = ["f00","f01","o00","o10","o20","r2","f10","f11","r3","o01","o11","o21"]
 T_ORDER = """
-gt F.1.1 F.0.0 F.4.0 F.2.1 F.4.1 F.3.1 F.6.1 F.5.1 F.0.1 F.2.0 F.1.0 F.9.0 AT.0.0.2 AT.0.0.1 AT.0.1.1 AT.0.1.2 F.3.0 T.1 T.2 AT.0.0.0 AT.0.1.0 F.7.0 T.0 AT.1.0.0 AT.1.0.1 T.3 AT.1.0.2 AT.1.1.1 AT.1.1.2 AT.1.1.0 T.4 F.5.0 F.6.0 F.7.1 F.10.1 F.8.0 S2.0.0.1 S2.0.0.0 F.9.1 F.8.1 S2.0.0.3 S2.0.0.2 S2.1.0.1 F.13.0 S2.1.0.3 S2.1.0.0 S2.1.0.2 F.12.1 F.11.0 T.5 S2.1.1.3 S2.0.1.0 F.11.1 S2.0.1.3 S2.0.1.1 S2.0.1.2 S2.1.1.0 F.10.0 T.6 T.8 T.7 T.9 F.13.1 S2.1.1.2 F.14.0 F.12.0 S2.1.1.1 S3.9.0 S3.3.0 S3.2.0 T.10 T.11 S3.1.0 S3.0.0 S3.2.1 F.15.0 S3.5.1 F.14.1 F.15.1 S3.9.1 S3.0.1 S3.1.1 S3.6.1 S3.3.1 T.12 T.13 S3.11.1 S3.4.1 S3.10.1 S3.8.0 S3.5.0 S3.6.0 T.15 T.14 S3.13.1 S3.7.1 S3.13.0 S3.10.0 S3.12.1 S3.11.0 S3.14.0 S3.15.0 S3.14.1 S3.4.0 S3.7.0 S3.15.1 S3.12.0 S3.8.1
+gt F.0.0 F.0.1 F.1.0 F.1.1 F.2.0 F.2.1 F.3.0 F.3.1 T.0 T.1 AT.0.0.0 T.2 F.4.0 F.4.1 AT.0.0.1
+AT.0.0.2 AT.0.1.0 AT.0.1.1 T.3 F.5.0 F.5.1 U.2.0.0 U.2.0.1 AT.0.1.2 AT.1.0.0 AT.1.0.1 AT.1.0.2 AT.1.1.0 U.2.0.2 U.2.0.3 F.6.0
+F.6.1 AT.1.1.1 AT.1.1.2 F.7.0 S2.0.0.0 F.7.1 S2.0.0.1 S2.0.0.2 T.4 T.5 T.6 S2.0.0.3 U.2.1.0 U.2.1.1 S2.1.0.0 S2.1.0.1
+S2.1.0.2 T.7 U.2.1.2 U.2.1.3 S2.1.0.3 S2.0.1.0 U.3.0.0 U.3.0.1 S2.0.1.1 U.3.0.2 U.3.0.3 S2.0.1.2 S2.0.1.3 S2.1.1.0 S2.1.1.1 S3.0.0
+S2.1.1.2 S2.1.1.3 U.3.1.0 U.3.1.1 S3.1.0 S3.2.0 S3.3.0 S3.4.0 U.3.1.2 S3.5.0 S3.6.0 S3.7.0 U.3.1.3 S3.0.1 S3.1.1 S3.2.1
+S3.3.1 S3.4.1 S3.5.1 S3.6.1 S3.7.1 S3.8.0 S3.9.0 S3.10.0 S3.11.0 S3.12.0 S3.13.0 S3.14.0 S3.15.0 S3.8.1 S3.9.1 S3.10.1
+S3.11.1 S3.12.1 S3.13.1 S3.14.1 S3.15.1
 """
 V_ORDER = """
-D.1.1 D.4.0 D.3.1 D.6.1 D.0.1 D.9.0 B.0.0 B.1.0 W.2 B.2.0 AQ.0.1 BQ.2.0 BQ.0.0 A.1.0.1 AQ.0.0 AQ.0.2 BQ.1.0 AQ.1.0 D.7.1 AQ.1.1 C.0.0.1 AQ.1.2 D.8.1 B.2.1 B.0.1 BQ.2.1 BQ.1.1 BQ.0.1 W.5 FQ.0 EQ.1.0 C.0.1.1 FQ.2 C.1.1.0 W.6 EQ.0.1 D.10.0 FQ.4 EQ.0.0 FQ.1 O.9.0 O.3.0 EQ.1.1 FQ.3 O.2.0 O.0.0 O.1.0 FQ.5 O.2.1 O.5.1 O.0.1 O.9.1 O.1.1 O.6.1 O.3.1 O.11.1 FQ.6 O.4.1 O.8.0 O.5.0 O.10.1 O.6.0 O.13.1 O.7.1 FQ.7 O.13.0 O.12.1 O.11.0 O.10.0 O.14.0 O.15.0 O.4.0 O.14.1 O.12.0 O.8.1 O.7.0 O.15.1
+P.0 P.1 D.0.0 D.1.1 D.2.0 D.3.0 D.3.1 FQ.0 B.0.0 B.1.0 B.2.0 BQ.0.0 AQ.0.0 Y.2.0.0 Y.2.0.1 BQ.1.0
+BQ.2.0 AQ.0.1 AQ.0.2 Y.2.0.2 Y.2.0.3 AQ.1.0 B.0.1 B.1.1 AQ.1.1 AQ.1.2 BQ.0.1 BQ.1.1 B.2.1 Y.2.1.0 Y.2.1.1 BQ.2.1
+Y.2.1.2 I.2.0 Y.2.1.3 Y.3.0.0 EQ.0.0 EQ.1.0 Y.3.0.1 Y.3.0.2 Y.3.0.3 FQ.1 TQ.2.0 EQ.0.1 O.0.0 TQ.2.1 FQ.2 FQ.3
+Y.3.1.0 TQ.3.0 O.1.0 Y.3.1.1 EQ.1.1 M.2.0 M.3.0 M.4.0 Y.3.1.2 M.5.0 M.6.0 M.7.0 Y.3.1.3 M.0.1 M.1.1 M.2.1
+O.3.1 O.4.1 O.5.1 O.6.1 TQ.3.1 M.7.1 M.8.0 M.9.0 O.10.0 O.11.0 M.12.0 M.13.0 O.15.0 M.14.0 O.8.1 O.11.1
+M.9.1 M.10.1 O.13.1 M.12.1 M.14.1 M.15.1
 """
 S_ORDER = """
-gs D.0.0 D.2.1 D.4.1 D.5.1 D.2.0 A.0.0.2 D.1.0 A.0.1.1 A.0.0.1 D.3.0 W.1 A.0.1.2 A.0.0.0 D.7.0 A.1.0.0 A.0.1.0 W.0 W.3 A.1.1.1 A.1.0.2 A.1.1.2 A.1.1.0 D.5.0 W.4 D.6.0 D.10.1 D.8.0 C.0.0.0 B.1.1 D.9.1 C.0.0.3 C.0.0.2 C.1.0.1 C.1.0.3 D.13.0 C.1.0.2 C.1.0.0 C.1.1.3 C.0.1.0 D.12.1 D.11.0 C.0.1.3 C.0.1.2 D.11.1 W.8 W.9 D.13.1 W.7 D.14.0 D.12.0 C.1.1.1 C.1.1.2 W.10 W.11 D.14.1 D.15.0 D.15.1 W.12 W.13 W.14 W.15
+gs D.0.1 D.1.0 D.2.1 W.0 W.1 W.2 A.0.0.0 D.4.0 D.4.1 A.0.0.1 A.0.0.2 A.0.1.0 A.0.1.1 X.2 W.3
+D.5.0 D.5.1 A.0.1.2 A.1.0.0 A.1.0.1 A.1.0.2 A.1.1.0 A.1.1.1 A.1.1.2 D.6.0 D.6.1 C.0.0.0 X.3 D.7.0 D.7.1 C.0.0.1
+C.0.0.2 W.4 W.5 W.6 C.0.0.3 W.7 C.1.0.0 C.1.0.1 C.1.0.2 C.1.0.3 C.0.1.0 I.2.1 C.0.1.1 C.0.1.2 C.0.1.3 C.1.1.0
+C.1.1.1 I.3.0 C.1.1.2 C.1.1.3 O.2.0 O.3.0 O.4.0 O.5.0 O.6.0 O.7.0 O.0.1 O.1.1 O.2.1 I.3.1 O.7.1 O.8.0
+O.9.0 O.12.0 O.13.0 O.14.0 O.9.1 O.10.1 O.12.1 O.14.1 O.15.1
 """
 
 
@@ -49,6 +66,10 @@ def tile_exponential_shadow_visibility_s12_kernel(
 
         atom_c = keep.tile([P, 2 * TEX], U8, name="atom_c", align_bytes=64)
         atom_s = keep.tile([P, TEX], U8, name="atom_s", align_bytes=64)
+        atom_pc = [keep.tile([P, 1024], U8, name=f"atom_pc{g}", align_bytes=64) for g in range(n_g)]
+        atom_ps = [keep.tile([P, 512], U8, name=f"atom_ps{g}", align_bytes=64) for g in range(n_g)]
+        recv_b = {q: keep.tile([P, 512], BF16, name=f"recv_b{q}") for q in TPQ}
+        gain_b = {q: keep.tile([P, 512], F32, name=f"gain_b{q}") for q in TPQ}
         foot_c = keep.tile([P, 2 * REC], U8, name="foot_c", align_bytes=64)
         foot_s = keep.tile([P, REC], U8, name="foot_s", align_bytes=64)
         ident = keep.tile([P, P], F32, name="ident")
@@ -65,7 +86,7 @@ def tile_exponential_shadow_visibility_s12_kernel(
         f_q = [keep.tile([P, 512], U32, name=f"f_q{k}", align_bytes=64) for k in range(n_rt // 2)]
         f_s = [keep.tile([P, 512], U8, name=f"f_s{k}", align_bytes=64) for k in range(n_rt // 2)]
         filt_x = [[keep.tile([P, 2, RAW], BF16, name=f"filt_x{g}{jp}") for jp in range(2)] for g in range(n_g)]
-        occ_x = [[keep.tile([P, 4, 512], BF16, name=f"occ_x{c}{h}") for h in range(2)] for c in range(n_c)]
+        occ_x = [[outs.tile([P, 2048], BF16, name=f"occ_x{c}{h}", tag="io") for h in range(2)] for c in range(n_c)]
         occ_k = [[None, None] for c in range(n_c)]
 
         nc.vector.memset(rows16[:], 0.0)
@@ -92,10 +113,13 @@ def tile_exponential_shadow_visibility_s12_kernel(
 
         def load_occ(c, h):
             src = occ[512 * c : 512 * (c + 1), :].rearrange("(p j) l -> p j l", j=4)
-            nc.sync.dma_start(out=occ_x[c][h][:], in_=src[:, :, 512 * h : 512 * (h + 1)])
+            nc.sync.dma_start(out=occ_x[c][h][:].rearrange("p (j l) -> p j l", j=4), in_=src[:, :, 512 * h : 512 * (h + 1)])
 
         for step in LOADS:
-            if step[0] == "f":
+            if step[0] == "r":
+                q = int(step[1])
+                nc.sync.dma_start(out=recv_b[q][:], in_=recv[512 * q : 512 * (q + 1)].partition_broadcast(P))
+            elif step[0] == "f":
                 load_filt(int(step[1]), int(step[2]))
             else:
                 load_occ(int(step[1]), int(step[2]))
@@ -140,12 +164,14 @@ def tile_exponential_shadow_visibility_s12_kernel(
         def fd(rt, g, engine):
             if rt not in f_nat:
                 f_nat[rt] = work.tile([P, TEX], BF16, name="nat", bufs=8)
-            dst = f_nat[rt][:, 512 * g : 512 * (g + 1)].rearrange("p (u w e) -> p u w e", u=2, e=2)
-            src = banks["f", rt, g][:].rearrange("p (w u e) -> p u w e", u=2, e=2)
-            if engine == "V":
-                nc.vector.tensor_scalar_mul(dst, src, gain[:, rt : rt + 1])
-            else:
-                nc.scalar.activation(dst, src, COPY, scale=gain[:, rt : rt + 1])
+            dst = f_nat[rt][:, 512 * g : 512 * (g + 1)].rearrange("p (u b i e) -> p u b i e", u=2, i=4, e=2)
+            src = banks["f", rt, g][:].rearrange("p (b u e i) -> p u b i e", u=2, i=4, e=2)
+            parts = [(dst, src)] if not SPLIT_D else [(dst[:, u], src[:, u]) for u in range(2)]
+            for d, s in parts:
+                if engine == "V":
+                    nc.vector.tensor_scalar_mul(d, s, gain[:, rt : rt + 1])
+                else:
+                    nc.scalar.activation(d, s, COPY, scale=gain[:, rt : rt + 1])
 
         def ft(rt):
             words = f_nat[rt][:].bitcast(F32)
@@ -167,6 +193,50 @@ def tile_exponential_shadow_visibility_s12_kernel(
         def fq(k):
             nc.vector.quantize_mx(out=f_q[k][:].bitcast(FP8X4), scales=f_s[k][:], in_=f_k[k][:])
 
+        w_t = {}
+
+        def atoms(g):
+            nc.vector.tensor_copy(
+                out=atom_pc[g][:].bitcast(I32).rearrange("p (t b w) -> p t b w", t=4, w=2),
+                in_=atom_c[:, 1024 * g : 1024 * (g + 1)].bitcast(I32).rearrange("p (b t w) -> p t b w", t=4, w=2),
+            )
+            nc.vector.tensor_copy(
+                out=atom_ps[g][:].bitcast(I32).rearrange("p (t b) -> p t b", t=4),
+                in_=atom_s[:, 512 * g : 512 * (g + 1)].bitcast(I32).rearrange("p (b t) -> p t b", t=4),
+            )
+
+        def gains(q):
+            nc.scalar.activation(gain_b[q][:], recv_b[q][:], EXP)
+
+        def u1(q, g, t):
+            nc.tensor.matmul_mx(
+                out=new_bank(("u", q, g, t))[:],
+                lhsT=atom_pc[g][:, 256 * t : 256 * (t + 1)].bitcast(FP4X4),
+                lhsT_scale=atom_ps[g][:, P * t : P * (t + 1)],
+                rhs=foot_c[:, 1024 * q : 1024 * (q + 1)].bitcast(FP4X4),
+                rhs_scale=foot_s[:, 512 * q : 512 * (q + 1)],
+                start=True,
+                stop=True,
+            )
+
+        def yd(q, g, t):
+            if (q, g) not in w_t:
+                w_t[q, g] = work.tile([P, 4, 512], BF16, name="w_t", bufs=2)
+            nc.vector.tensor_tensor(out=w_t[q, g][:, t, :], in0=banks["u", q, g, t][:], in1=gain_b[q][:], op=mybir.AluOpType.mult)
+
+        def fi(q, g, engine):
+            f_k[q, g] = work.tile([P, 2048], BF16, name="f_kt", bufs=4, align_bytes=64)
+            dst = f_k[q, g][:].rearrange("p (n t) -> p n t", t=4)
+            src = w_t[q, g][:].rearrange("p t n -> p n t")
+            if engine == "V":
+                nc.vector.tensor_copy(out=dst, in_=src)
+            else:
+                nc.scalar.copy(dst, src)
+
+        def tq(q, g):
+            k = 2 * q + g
+            nc.vector.quantize_mx(out=f_q[k][:].bitcast(FP8X4), scales=f_s[k][:], in_=f_k[q, g][:])
+
         filt_k = {}
 
         def at(g, jp, c):
@@ -180,9 +250,9 @@ def tile_exponential_shadow_visibility_s12_kernel(
 
         def ac(g, jp, c, engine):
             if (g, c) not in filt_k:
-                filt_k[g, c] = work.tile([P, 2048], BF16, name="filt_k", bufs=6, align_bytes=64)
-            dst = filt_k[g, c][:, 1024 * jp : 1024 * (jp + 1)].bitcast(F32).rearrange("p (j m u) -> p j m u", j=2, u=2)
-            src = banks["a", g, jp, c][:].rearrange("p (j u m) -> p j m u", j=2, u=2)
+                filt_k[g, c] = work.tile([P, 2048], BF16, name="filt_k", bufs=5, align_bytes=64)
+            dst = filt_k[g, c][:].bitcast(F32).rearrange("p (t b x) -> p t b x", t=4, x=8)[:, :, :, 4 * jp : 4 * jp + 4]
+            src = banks["a", g, jp, c][:].rearrange("p (x b t) -> p t b x", t=4, x=4)
             if engine == "V":
                 nc.vector.tensor_copy(out=dst, in_=src)
             else:
@@ -192,9 +262,9 @@ def tile_exponential_shadow_visibility_s12_kernel(
             nc.vector.quantize_mx(out=filt_q[g][c][:].bitcast(FP8X4), scales=filt_s[g][c][:], in_=filt_k[g, c][:])
 
         def bi(c, h, engine):
-            occ_k[c][h] = work.tile([P, 2048], BF16, name="occ_kt", bufs=6, align_bytes=64)
+            occ_k[c][h] = work.tile([P, 2048], BF16, name="occ_kt", bufs=4, align_bytes=64)
             dst = occ_k[c][h][:].rearrange("p (l j) -> p l j", j=4)
-            src = occ_x[c][h][:].rearrange("p j l -> p l j")
+            src = occ_x[c][h][:].rearrange("p (j l) -> p l j", j=4)
             if engine == "V":
                 nc.vector.tensor_copy(out=dst, in_=src)
             else:
@@ -238,7 +308,11 @@ def tile_exponential_shadow_visibility_s12_kernel(
             k, i = rt // 2, rt % 2
             bank = new_bank(("o", rt, h))
             for g in range(n_g):
-                cols = slice(P * (2 * i + g), P * (2 * i + g + 1))
+                if rt // 4 in TPQ:
+                    k, j = 2 * (rt // 4) + g, rt % 4
+                else:
+                    k, j = rt // 2, 2 * i + g
+                cols = slice(P * j, P * (j + 1))
                 nc.tensor.matmul_mx(
                     out=bank[:],
                     lhsT=f_q[k][:, cols].bitcast(FP8X4),
@@ -250,8 +324,9 @@ def tile_exponential_shadow_visibility_s12_kernel(
                 )
 
         def od(rt, h, engine):
-            out_t[rt, h] = outs.tile([P, 512], F32, name="out_t")
-            dst = out_t[rt, h][:]
+            if (rt // 2, h) not in out_t:
+                out_t[rt // 2, h] = outs.tile([P, 1024], F32, name="out_t", tag="io")
+            dst = out_t[rt // 2, h][:, 512 * (rt % 2) : 512 * (rt % 2 + 1)]
             if engine == "V":
                 nc.vector.tensor_scalar_min(dst, banks["o", rt, h][:], 1.0)
                 nc.sync.dma_start(out=out[P * rt : P * (rt + 1), 512 * h : 512 * (h + 1)], in_=dst)
@@ -259,7 +334,7 @@ def tile_exponential_shadow_visibility_s12_kernel(
                 nc.scalar.copy(dst, banks["o", rt, h][:])
 
         def om(rt, h):
-            dst = out_t[rt, h][:]
+            dst = out_t[rt // 2, h][:, 512 * (rt % 2) : 512 * (rt % 2 + 1)]
             nc.vector.tensor_scalar_min(dst, dst, 1.0)
             nc.sync.dma_start(out=out[P * rt : P * (rt + 1), 512 * h : 512 * (h + 1)], in_=dst)
 
@@ -299,9 +374,22 @@ def tile_exponential_shadow_visibility_s12_kernel(
             if k == "EQ":
                 return ["C.%d.%d.%d" % (n[0], n[1], i) for i in range(4)], lambda: eq(*n)
             if k == "S3":
-                return ["FQ.%d" % (n[0] // 2)] + ["EQ.%d.%d" % (g, n[1]) for g in range(2)], lambda: s3(*n)
+                fd_ = ["TQ.%d.%d" % (n[0] // 4, g) for g in range(2)] if n[0] // 4 in TPQ else ["FQ.%d" % (n[0] // 2)]
+                return fd_ + ["EQ.%d.%d" % (g, n[1]) for g in range(2)], lambda: s3(*n)
             if k == "O":
                 return ["S3.%d.%d" % (n[0], n[1])], lambda: od(n[0], n[1], e)
+            if k == "P":
+                return [], lambda: atoms(*n)
+            if k == "X":
+                return [], lambda: gains(*n)
+            if k == "U":
+                return ["P.%d" % n[1]], lambda: u1(*n)
+            if k == "Y":
+                return ["X.%d" % n[0], "U.%d.%d.%d" % (n[0], n[1], n[2])], lambda: yd(*n)
+            if k == "I":
+                return ["Y.%d.%d.%d" % (n[0], n[1], t) for t in range(4)], lambda: fi(n[0], n[1], e)
+            if k == "TQ":
+                return ["I.%d.%d" % (n[0], n[1])], lambda: tq(*n)
             if k == "M":
                 return ["O.%d.%d" % (n[0], n[1])], lambda: om(*n)
             raise ValueError(token)

@@ -22,30 +22,30 @@ BANK = 512
 TPQ = (2, 3,)
 SPLIT_D = True
 
-LOADS = ["f00","f01","o00","o10","o20","r2","f10","f11","r3","o01","o11","o21"]
+LOADS = ["f01","o00","o10","o20","f10","f11","o01","o11","o21"]
 T_ORDER = """
-gt F.0.0 F.0.1 F.1.0 F.1.1 F.2.0 F.2.1 F.3.0 F.3.1 T.0 T.1 AT.0.0.0 T.2 F.4.0 F.4.1 AT.0.0.1
-AT.0.0.2 AT.0.1.0 AT.0.1.1 T.3 F.5.0 F.5.1 U.2.0.0 U.2.0.1 AT.0.1.2 AT.1.0.0 AT.1.0.1 AT.1.0.2 AT.1.1.0 U.2.0.2 U.2.0.3 F.6.0
-F.6.1 AT.1.1.1 AT.1.1.2 F.7.0 S2.0.0.0 F.7.1 S2.0.0.1 S2.0.0.2 T.4 T.5 T.6 S2.0.0.3 U.2.1.0 U.2.1.1 S2.1.0.0 S2.1.0.1
-S2.1.0.2 T.7 U.2.1.2 U.2.1.3 S2.1.0.3 S2.0.1.0 U.3.0.0 U.3.0.1 S2.0.1.1 U.3.0.2 U.3.0.3 S2.0.1.2 S2.0.1.3 S2.1.1.0 S2.1.1.1 S3.0.0
-S2.1.1.2 S2.1.1.3 U.3.1.0 U.3.1.1 S3.1.0 S3.2.0 S3.3.0 S3.4.0 U.3.1.2 S3.5.0 S3.6.0 S3.7.0 U.3.1.3 S3.0.1 S3.1.1 S3.2.1
-S3.3.1 S3.4.1 S3.5.1 S3.6.1 S3.7.1 S3.8.0 S3.9.0 S3.10.0 S3.11.0 S3.12.0 S3.13.0 S3.14.0 S3.15.0 S3.8.1 S3.9.1 S3.10.1
-S3.11.1 S3.12.1 S3.13.1 S3.14.1 S3.15.1
+AT.0.0.0 AT.0.0.1 gt F.0.0 F.0.1 F.1.0 F.1.1 F.2.0 AT.0.0.2 AT.0.1.0 T.0 GB.2 AT.0.1.1 F.2.1 F.3.0 GB.3
+AT.0.1.2 U.2.0.0 F.3.1 AT.1.0.0 AT.1.0.1 U.2.0.1 U.2.0.2 AT.1.0.2 AT.1.1.0 AT.1.1.1 T.1 U.2.0.3 F.4.0 F.4.1 U.2.1.0 T.2
+AT.1.1.2 T.3 S2.0.0.0 U.2.1.1 S2.0.0.1 S2.0.0.2 S2.0.0.3 U.2.1.2 F.5.0 U.2.1.3 S2.1.0.0 S2.1.0.1 S2.1.0.2 F.5.1 T.4 S2.1.0.3
+S2.0.1.0 U.3.0.0 U.3.0.1 F.6.0 S2.0.1.1 F.6.1 S2.0.1.2 U.3.0.2 S2.0.1.3 F.7.0 U.3.0.3 U.3.1.0 U.3.1.1 F.7.1 U.3.1.2 S3.0.0
+T.5 T.6 T.7 S2.1.1.0 S2.1.1.1 U.3.1.3 S3.1.0 S3.2.0 S3.3.0 S2.1.1.2 S2.1.1.3 S3.4.0 S3.5.0 S3.6.0 S3.7.0 S3.0.1
+S3.1.1 S3.2.1 S3.3.1 S3.4.1 S3.5.1 S3.6.1 S3.7.1 S3.8.0 S3.9.0 S3.10.0 S3.11.0 S3.12.0 S3.13.0 S3.14.0 S3.15.0 S3.8.1
+S3.9.1 S3.10.1 S3.11.1 S3.12.1 S3.13.1 S3.14.1 S3.15.1
 """
 V_ORDER = """
-P.0 P.1 D.0.0 D.1.1 D.2.0 D.3.0 D.3.1 FQ.0 B.0.0 B.1.0 B.2.0 BQ.0.0 AQ.0.0 Y.2.0.0 Y.2.0.1 BQ.1.0
-BQ.2.0 AQ.0.1 AQ.0.2 Y.2.0.2 Y.2.0.3 AQ.1.0 B.0.1 B.1.1 AQ.1.1 AQ.1.2 BQ.0.1 BQ.1.1 B.2.1 Y.2.1.0 Y.2.1.1 BQ.2.1
-Y.2.1.2 I.2.0 Y.2.1.3 Y.3.0.0 EQ.0.0 EQ.1.0 Y.3.0.1 Y.3.0.2 Y.3.0.3 FQ.1 TQ.2.0 EQ.0.1 O.0.0 TQ.2.1 FQ.2 FQ.3
-Y.3.1.0 TQ.3.0 O.1.0 Y.3.1.1 EQ.1.1 M.2.0 M.3.0 M.4.0 Y.3.1.2 M.5.0 M.6.0 M.7.0 Y.3.1.3 M.0.1 M.1.1 M.2.1
-O.3.1 O.4.1 O.5.1 O.6.1 TQ.3.1 M.7.1 M.8.0 M.9.0 O.10.0 O.11.0 M.12.0 M.13.0 O.15.0 M.14.0 O.8.1 O.11.1
-M.9.1 M.10.1 O.13.1 M.12.1 M.14.1 M.15.1
+A.0.0.0 P.0 P.1 D.0.1 D.1.0 B.0.0 B.1.0 B.2.0 AQ.0.0 AQ.0.1 Y.2.0.0 BQ.0.0 BQ.1.0 Y.2.0.1 Y.2.0.2 BQ.2.0
+AQ.0.2 Y.2.0.3 Y.2.1.0 AQ.1.0 AQ.1.1 AQ.1.2 Y.2.1.1 FQ.0 B.0.1 B.1.1 Y.2.1.2 BQ.0.1 BQ.1.1 BQ.2.1 Y.2.1.3 I.2.0
+I.2.1 Y.3.0.0 Y.3.0.1 FQ.1 EQ.0.0 EQ.1.0 Y.3.0.2 Y.3.0.3 Y.3.1.0 TQ.2.0 Y.3.1.1 O.0.0 Y.3.1.2 TQ.2.1 FQ.2 FQ.3
+O.1.0 O.2.0 EQ.0.1 Y.3.1.3 M.3.0 TQ.3.0 EQ.1.1 M.4.0 O.5.0 O.6.0 O.7.0 O.0.1 O.1.1 M.2.1 O.4.1 M.3.1
+M.5.1 TQ.3.1 M.6.1 M.7.1 M.8.0 M.9.0 M.10.0 M.11.0 O.12.0 M.13.0 M.14.0 M.15.0 M.8.1 M.9.1 M.10.1 O.13.1
+M.11.1 M.12.1 M.14.1 M.15.1
 """
 S_ORDER = """
-gs D.0.1 D.1.0 D.2.1 W.0 W.1 W.2 A.0.0.0 D.4.0 D.4.1 A.0.0.1 A.0.0.2 A.0.1.0 A.0.1.1 X.2 W.3
-D.5.0 D.5.1 A.0.1.2 A.1.0.0 A.1.0.1 A.1.0.2 A.1.1.0 A.1.1.1 A.1.1.2 D.6.0 D.6.1 C.0.0.0 X.3 D.7.0 D.7.1 C.0.0.1
-C.0.0.2 W.4 W.5 W.6 C.0.0.3 W.7 C.1.0.0 C.1.0.1 C.1.0.2 C.1.0.3 C.0.1.0 I.2.1 C.0.1.1 C.0.1.2 C.0.1.3 C.1.1.0
-C.1.1.1 I.3.0 C.1.1.2 C.1.1.3 O.2.0 O.3.0 O.4.0 O.5.0 O.6.0 O.7.0 O.0.1 O.1.1 O.2.1 I.3.1 O.7.1 O.8.0
-O.9.0 O.12.0 O.13.0 O.14.0 O.9.1 O.10.1 O.12.1 O.14.1 O.15.1
+A.0.0.1 gs D.0.0 D.1.1 D.2.0 A.0.0.2 A.0.1.0 W.0 X.2 A.0.1.1 D.2.1 X.3 D.3.0 A.0.1.2 D.3.1 A.1.0.0
+A.1.0.1 A.1.0.2 A.1.1.0 A.1.1.1 W.1 D.4.0 A.1.1.2 D.4.1 W.2 W.3 C.0.0.0 C.0.0.1 B.2.1 C.0.0.2 C.0.0.3 C.1.0.0
+D.5.0 C.1.0.1 C.1.0.2 D.5.1 W.4 D.6.0 C.1.0.3 C.0.1.0 D.6.1 C.0.1.1 C.0.1.2 C.0.1.3 D.7.0 D.7.1 W.5 W.6
+W.7 I.3.0 C.1.1.0 C.1.1.1 O.3.0 C.1.1.2 C.1.1.3 O.4.0 I.3.1 O.2.1 O.3.1 O.5.1 O.6.1 O.7.1 O.8.0 O.9.0
+O.10.0 O.11.0 O.13.0 O.14.0 O.15.0 O.8.1 O.9.1 O.10.1 O.11.1 O.12.1 O.14.1 O.15.1
 """
 
 
@@ -68,7 +68,6 @@ def tile_exponential_shadow_visibility_s12_kernel(
         atom_s = keep.tile([P, TEX], U8, name="atom_s", align_bytes=64)
         atom_pc = [keep.tile([P, 1024], U8, name=f"atom_pc{g}", align_bytes=64) for g in range(n_g)]
         atom_ps = [keep.tile([P, 512], U8, name=f"atom_ps{g}", align_bytes=64) for g in range(n_g)]
-        recv_b = {q: keep.tile([P, 512], BF16, name=f"recv_b{q}") for q in TPQ}
         gain_b = {q: keep.tile([P, 512], F32, name=f"gain_b{q}") for q in TPQ}
         foot_c = keep.tile([P, 2 * REC], U8, name="foot_c", align_bytes=64)
         foot_s = keep.tile([P, REC], U8, name="foot_s", align_bytes=64)
@@ -93,19 +92,10 @@ def tile_exponential_shadow_visibility_s12_kernel(
         nc.vector.memset(atom_s[:].bitcast(I32), 0)
         nc.vector.memset(foot_s[:].bitcast(I32), 0)
         nc.vector.memset(warm[:], 0.0)
-        nc.sync.dma_start(out=atom_c[:].bitcast(I32), in_=atom_words[0].bitcast(I32))
-        nc.sync.dma_start(out=foot_c[:].bitcast(I32), in_=foot_words[0].bitcast(I32))
-        nc.gpsimd.dma_start(out=rows16[0:n_rt, :], in_=recv.rearrange("(c n) -> c n", n=P))
-        for q in range(4):
-            nc.scalar.dma_start(
-                out=atom_s[32 * q : 32 * q + 4, :].bitcast(I32), in_=atom_scales[0][4 * q : 4 * q + 4, :].bitcast(I32)
-            )
-        for q in range(4):
-            (nc.scalar if q < 2 else nc.gpsimd).dma_start(
-                out=foot_s[32 * q : 32 * q + 4, :].bitcast(I32), in_=foot_scales[0][4 * q : 4 * q + 4, :].bitcast(I32)
-            )
-        make_identity(nc, ident[:])
-        nc.scalar.activation(warm[:], warm[:], EXP)
+        nc.vector.memset(ident[:], 0.0)
+        nc.gpsimd.affine_select(
+            out=ident[:], in_=ident[:], pattern=[[-1, P]], compare_op=mybir.AluOpType.not_equal, fill=1.0, base=0, channel_multiplier=1
+        )
 
         def load_filt(g, jp):
             src = filt[512 * g : 512 * (g + 1), :].rearrange("(m j) k -> m j k", j=4)
@@ -115,11 +105,21 @@ def tile_exponential_shadow_visibility_s12_kernel(
             src = occ[512 * c : 512 * (c + 1), :].rearrange("(p j) l -> p j l", j=4)
             nc.sync.dma_start(out=occ_x[c][h][:].rearrange("p (j l) -> p j l", j=4), in_=src[:, :, 512 * h : 512 * (h + 1)])
 
+        load_filt(0, 0)
+        nc.sync.dma_start(out=atom_c[:].bitcast(I32), in_=atom_words[0].bitcast(I32))
+        nc.sync.dma_start(out=foot_c[:].bitcast(I32), in_=foot_words[0].bitcast(I32))
+        nc.gpsimd.dma_start(out=rows16[0:n_rt, :], in_=recv.rearrange("(c n) -> c n", n=P))
+        for q in range(4):
+            nc.scalar.dma_start(
+                out=atom_s[32 * q : 32 * q + 4, :].bitcast(I32), in_=atom_scales[0][4 * q : 4 * q + 4, :].bitcast(I32)
+            )
+        for q in range(4):
+            (nc.scalar if q < 1 else nc.sync if q < 3 else nc.gpsimd).dma_start(
+                out=foot_s[32 * q : 32 * q + 4, :].bitcast(I32), in_=foot_scales[0][4 * q : 4 * q + 4, :].bitcast(I32)
+            )
+        nc.scalar.activation(warm[:], warm[:], EXP)
         for step in LOADS:
-            if step[0] == "r":
-                q = int(step[1])
-                nc.sync.dma_start(out=recv_b[q][:], in_=recv[512 * q : 512 * (q + 1)].partition_broadcast(P))
-            elif step[0] == "f":
+            if step[0] == "f":
                 load_filt(int(step[1]), int(step[2]))
             else:
                 load_occ(int(step[1]), int(step[2]))
@@ -205,8 +205,14 @@ def tile_exponential_shadow_visibility_s12_kernel(
                 in_=atom_s[:, 512 * g : 512 * (g + 1)].bitcast(I32).rearrange("p (b t) -> p t b", t=4),
             )
 
+        def gain_cols(q):
+            bank = new_bank(("g", q))
+            for i in range(4):
+                rt = 4 * q + i
+                nc.tensor.transpose(bank[:, P * i : P * (i + 1)], gain[:, rt : rt + 1].to_broadcast([P, P]), ident[:])
+
         def gains(q):
-            nc.scalar.activation(gain_b[q][:], recv_b[q][:], EXP)
+            nc.scalar.copy(gain_b[q][:], banks["g", q][:])
 
         def u1(q, g, t):
             nc.tensor.matmul_mx(
@@ -226,8 +232,8 @@ def tile_exponential_shadow_visibility_s12_kernel(
 
         def fi(q, g, engine):
             f_k[q, g] = work.tile([P, 2048], BF16, name="f_kt", bufs=4, align_bytes=64)
-            dst = f_k[q, g][:].rearrange("p (n t) -> p n t", t=4)
-            src = w_t[q, g][:].rearrange("p t n -> p n t")
+            dst = f_k[q, g][:].rearrange("p (c i t) -> p c t i", i=4, t=4)
+            src = w_t[q, g][:].rearrange("p t (c i) -> p c t i", i=4)
             if engine == "V":
                 nc.vector.tensor_copy(out=dst, in_=src)
             else:
@@ -263,8 +269,8 @@ def tile_exponential_shadow_visibility_s12_kernel(
 
         def bi(c, h, engine):
             occ_k[c][h] = work.tile([P, 2048], BF16, name="occ_kt", bufs=4, align_bytes=64)
-            dst = occ_k[c][h][:].rearrange("p (l j) -> p l j", j=4)
-            src = occ_x[c][h][:].rearrange("p (j l) -> p l j", j=4)
+            dst = occ_k[c][h][:].rearrange("p (c i j) -> p c j i", i=4, j=4)
+            src = occ_x[c][h][:].rearrange("p (j c i) -> p c j i", j=4, i=4)
             if engine == "V":
                 nc.vector.tensor_copy(out=dst, in_=src)
             else:
@@ -380,8 +386,10 @@ def tile_exponential_shadow_visibility_s12_kernel(
                 return ["S3.%d.%d" % (n[0], n[1])], lambda: od(n[0], n[1], e)
             if k == "P":
                 return [], lambda: atoms(*n)
+            if k == "GB":
+                return ["gs"], lambda: gain_cols(*n)
             if k == "X":
-                return [], lambda: gains(*n)
+                return ["GB.%d" % n[0]], lambda: gains(*n)
             if k == "U":
                 return ["P.%d" % n[1]], lambda: u1(*n)
             if k == "Y":

@@ -1,7 +1,6 @@
 from contextlib import ExitStack
 
 import concourse.mybir as mybir
-from concourse.masks import make_identity
 
 REC, CODES, TEX, RAW, FRM = 2048, 512, 1024, 1536, 1024
 
@@ -16,36 +15,54 @@ FP8X4 = mybir.dt.float8_e4m3fn_x4
 FP4X4 = mybir.dt.float4_e2m1fn_x4
 COPY = mybir.ActivationFunctionType.Copy
 EXP = mybir.ActivationFunctionType.Exp
+MULT = mybir.AluOpType.mult
+NOT_EQUAL = mybir.AluOpType.not_equal
 
 P = 128
 BANK = 512
-TPQ = (2, 3,)
-SPLIT_D = True
+N_TILES = REC // P
+N_GROUPS = TEX // 512
+N_CHUNKS = RAW // 512
+LAST_TILE = N_TILES - 1
 
-LOADS = ["f01","o00","o10","o20","f10","f11","o01","o11","o21"]
-T_ORDER = """
-AT.0.0.0 AT.0.0.1 gt F.0.0 F.0.1 F.1.0 F.1.1 F.2.0 AT.0.0.2 AT.0.1.0 T.0 GB.2 AT.0.1.1 F.2.1 F.3.0 GB.3
-AT.0.1.2 U.2.0.0 F.3.1 AT.1.0.0 AT.1.0.1 U.2.0.1 U.2.0.2 AT.1.0.2 AT.1.1.0 AT.1.1.1 T.1 U.2.0.3 F.4.0 F.4.1 U.2.1.0 T.2
-AT.1.1.2 T.3 S2.0.0.0 U.2.1.1 S2.0.0.1 S2.0.0.2 S2.0.0.3 U.2.1.2 F.5.0 U.2.1.3 S2.1.0.0 S2.1.0.1 S2.1.0.2 F.5.1 T.4 S2.1.0.3
-S2.0.1.0 U.3.0.0 U.3.0.1 F.6.0 S2.0.1.1 F.6.1 S2.0.1.2 U.3.0.2 S2.0.1.3 F.7.0 U.3.0.3 U.3.1.0 U.3.1.1 F.7.1 U.3.1.2 S3.0.0
-T.5 T.6 T.7 S2.1.1.0 S2.1.1.1 U.3.1.3 S3.1.0 S3.2.0 S3.3.0 S2.1.1.2 S2.1.1.3 S3.4.0 S3.5.0 S3.6.0 S3.7.0 S3.0.1
-S3.1.1 S3.2.1 S3.3.1 S3.4.1 S3.5.1 S3.6.1 S3.7.1 S3.8.0 S3.9.0 S3.10.0 S3.11.0 S3.12.0 S3.13.0 S3.14.0 S3.15.0 S3.8.1
-S3.9.1 S3.10.1 S3.11.1 S3.12.1 S3.13.1 S3.14.1 S3.15.1
+COLUMN_QUADS = (0, 2)
+
+LATER_LOADS = (("occ", 0, 0), ("occ", 1, 0), ("occ", 2, 0), ("filt", 1, 0), ("filt", 1, 1), ("occ", 0, 1), ("occ", 1, 1), ("occ", 2, 1))
+
+TENSOR_ORDER = """
+FiltT.0.0.0 FiltT.0.0.1 FiltT.0.0.2 RecvT GainT.0 RowMM.4.0 RowMM.4.1 RowMM.5.0 ColMM.0.0.0 RowMM.5.1
+RowMM.6.0 FiltT.0.1.0 GainT.2 FiltT.0.1.1 FiltT.0.1.2 ColMM.0.0.1 RowMM.6.1 FiltT.1.0.0 FiltT.1.0.1
+FiltT.1.0.2 ColMM.0.0.2 RowMM.7.0 RowMM.7.1 ColMM.0.0.3 ColMM.0.1.0 RowT.4 FiltT.1.1.0 FiltT.1.1.1 FiltT.1.1.2
+RowT.5 ColMM.0.1.1 MapMM.0.0.0 MapMM.0.0.1 MapMM.0.0.2 MapMM.0.0.3 MapMM.1.0.0 ColMM.0.1.2 MapMM.1.0.1
+ColMM.0.1.3 MapMM.1.0.2 MapMM.1.0.3 ColMM.2.0.0 ColMM.2.0.1 MapMM.0.1.0 ColMM.2.0.2 MapMM.0.1.1 MapMM.0.1.2
+ColMM.2.0.3 MapMM.0.1.3 ColMM.2.1.0 MapMM.1.1.0 MapMM.1.1.1 RowMM.12.0 ColMM.2.1.1 MapMM.1.1.2 MapMM.1.1.3
+ColMM.2.1.2 ColMM.2.1.3 OutMM.0.0 RowT.6 RowT.7 RowMM.12.1 RowMM.13.0 OutMM.0.1 OutMM.1.0 OutMM.1.1 OutMM.2.0
+OutMM.2.1 OutMM.3.0 OutMM.3.1 OutMM.4.0 OutMM.4.1 RowMM.13.1 RowMM.14.0 RowMM.14.1 OutMM.5.0 OutMM.5.1
+RowMM.15.0 RowMM.15.1 OutMM.6.0 OutMM.6.1 OutMM.7.0 OutMM.7.1 OutMM.8.0 OutMM.8.1 RowT.12 RowT.13 RowT.14
+RowT.15 OutMM.9.0 OutMM.9.1 OutMM.10.0 OutMM.10.1 OutMM.11.0 OutMM.11.1 OutMM.12.0 OutMM.12.1 OutMM.13.0
+OutMM.13.1 OutMM.14.0 OutMM.14.1 OutMM.15.0 OutMM.15.1
 """
-V_ORDER = """
-A.0.0.0 P.0 P.1 D.0.1 D.1.0 B.0.0 B.1.0 B.2.0 AQ.0.0 AQ.0.1 Y.2.0.0 BQ.0.0 BQ.1.0 Y.2.0.1 Y.2.0.2 BQ.2.0
-AQ.0.2 Y.2.0.3 Y.2.1.0 AQ.1.0 AQ.1.1 AQ.1.2 Y.2.1.1 FQ.0 B.0.1 B.1.1 Y.2.1.2 BQ.0.1 BQ.1.1 BQ.2.1 Y.2.1.3 I.2.0
-I.2.1 Y.3.0.0 Y.3.0.1 FQ.1 EQ.0.0 EQ.1.0 Y.3.0.2 Y.3.0.3 Y.3.1.0 TQ.2.0 Y.3.1.1 O.0.0 Y.3.1.2 TQ.2.1 FQ.2 FQ.3
-O.1.0 O.2.0 EQ.0.1 Y.3.1.3 M.3.0 TQ.3.0 EQ.1.1 M.4.0 O.5.0 O.6.0 O.7.0 O.0.1 O.1.1 M.2.1 O.4.1 M.3.1
-M.5.1 TQ.3.1 M.6.1 M.7.1 M.8.0 M.9.0 M.10.0 M.11.0 O.12.0 M.13.0 M.14.0 M.15.0 M.8.1 M.9.1 M.10.1 O.13.1
-M.11.1 M.12.1 M.14.1 M.15.1
+VECTOR_ORDER = """
+FiltPack.0.0.0 AtomOrder.0 AtomOrder.1 FiltPack.0.0.1 FiltPack.0.0.2 OccPack.0.0 OccPack.1.0 ColGain.0.0.0
+OccQ.0.0 OccPack.2.0 FiltQ.0.0 ColGain.0.0.1 FiltQ.0.1 FiltQ.0.2 ColGain.0.0.2 OccQ.1.0 OccQ.2.0 ColGain.0.0.3
+ColGain.0.1.0 ColGain.0.1.1 FiltQ.1.0 FiltQ.1.1 FiltQ.1.2 OccPack.0.1 OccPack.1.1 OccQ.0.1 OccQ.1.1 OccQ.2.1
+ColGain.0.1.2 ColPack.0.0 ColGain.0.1.3 ColGain.2.0.0 ColGain.2.0.1 ColGain.2.0.2 ColGain.2.0.3 ColQ.0.0
+MapQ.0.0 ColGain.2.1.0 MapQ.1.0 MapQ.0.1 ColQ.0.1 RowQ.2 ColGain.2.1.1 ColGain.2.1.2 MapQ.1.1 ColGain.2.1.3
+OutCopy.0.0 OutCopy.0.1 OutCopy.1.0 OutCopy.1.1 OutCopy.2.0 RowQ.3 OutCopy.2.1 OutCopy.3.0 OutCopy.3.1
+OutCopy.4.0 OutCopy.4.1 ColQ.2.0 OutCopy.5.0 ColQ.2.1 OutCopy.5.1 OutCopy.6.0 OutCopy.6.1 OutCopy.7.0
+OutCopy.8.0 OutMin.7.1 OutMin.8.1 OutCopy.9.0 RowQ.6 OutMin.9.1 OutCopy.10.1 OutMin.10.0 OutCopy.11.1
+OutMin.11.0 RowQ.7 OutMin.12.0 OutMin.12.1 OutCopy.13.1 OutMin.13.0 OutCopy.14.1 OutMin.14.0 OutCopy.15.1
+OutMin.15.0
 """
-S_ORDER = """
-A.0.0.1 gs D.0.0 D.1.1 D.2.0 A.0.0.2 A.0.1.0 W.0 X.2 A.0.1.1 D.2.1 X.3 D.3.0 A.0.1.2 D.3.1 A.1.0.0
-A.1.0.1 A.1.0.2 A.1.1.0 A.1.1.1 W.1 D.4.0 A.1.1.2 D.4.1 W.2 W.3 C.0.0.0 C.0.0.1 B.2.1 C.0.0.2 C.0.0.3 C.1.0.0
-D.5.0 C.1.0.1 C.1.0.2 D.5.1 W.4 D.6.0 C.1.0.3 C.0.1.0 D.6.1 C.0.1.1 C.0.1.2 C.0.1.3 D.7.0 D.7.1 W.5 W.6
-W.7 I.3.0 C.1.1.0 C.1.1.1 O.3.0 C.1.1.2 C.1.1.3 O.4.0 I.3.1 O.2.1 O.3.1 O.5.1 O.6.1 O.7.1 O.8.0 O.9.0
-O.10.0 O.11.0 O.13.0 O.14.0 O.15.0 O.8.1 O.9.1 O.10.1 O.11.1 O.12.1 O.14.1 O.15.1
+SCALAR_ORDER = """
+Gain GainRow.0 RowGain.4.0 RowGain.4.1 RowGain.5.0 RowGain.5.1 RowGain.6.0 FiltPack.0.1.0 FiltPack.0.1.1
+GainRow.2 RowGain.6.1 FiltPack.0.1.2 FiltPack.1.0.0 FiltPack.1.0.1 FiltPack.1.0.2 RowGain.7.0 RowGain.7.1
+RowPack.4 FiltPack.1.1.0 FiltPack.1.1.1 FiltPack.1.1.2 RowPack.5 OccPack.2.1 MapPack.0.0.0 MapPack.0.0.1
+MapPack.0.0.2 MapPack.0.0.3 MapPack.1.0.0 MapPack.1.0.1 MapPack.1.0.2 MapPack.1.0.3 MapPack.0.1.0 ColPack.0.1
+MapPack.0.1.1 MapPack.0.1.2 MapPack.0.1.3 MapPack.1.1.0 MapPack.1.1.1 RowGain.12.0 MapPack.1.1.2 MapPack.1.1.3
+ColPack.2.0 RowPack.6 RowPack.7 RowGain.12.1 RowGain.13.0 ColPack.2.1 RowGain.13.1 RowGain.14.0 RowGain.14.1
+RowGain.15.0 RowGain.15.1 OutCopy.7.1 OutCopy.8.1 RowPack.12 RowPack.13 RowPack.14 OutCopy.9.1 OutCopy.10.0
+RowPack.15 OutCopy.11.0 OutCopy.12.0 OutCopy.12.1 OutCopy.13.0 OutCopy.14.0 OutCopy.15.0
 """
 
 
@@ -53,238 +70,234 @@ def tile_exponential_shadow_visibility_s12_kernel(
     tc, foot_words, foot_scales, atom_words, atom_scales, filt, occ, recv, out
 ):
     nc = tc.nc
-    n_rt = REC // P
-    n_g = TEX // 512
-    n_c = RAW // 512
 
     with ExitStack() as ctx:
         keep = ctx.enter_context(tc.tile_pool(name="keep", bufs=1))
         work = ctx.enter_context(tc.tile_pool(name="work", bufs=3))
-        outs = ctx.enter_context(tc.tile_pool(name="outs", bufs=10))
+        ring = ctx.enter_context(tc.tile_pool(name="ring", bufs=10))
         psum = ctx.enter_context(tc.psum_pool(name="psum", bufs=8))
         ctx.enter_context(tc.manual_schedule())
 
         atom_c = keep.tile([P, 2 * TEX], U8, name="atom_c", align_bytes=64)
         atom_s = keep.tile([P, TEX], U8, name="atom_s", align_bytes=64)
-        atom_pc = [keep.tile([P, 1024], U8, name=f"atom_pc{g}", align_bytes=64) for g in range(n_g)]
-        atom_ps = [keep.tile([P, 512], U8, name=f"atom_ps{g}", align_bytes=64) for g in range(n_g)]
-        gain_b = {q: keep.tile([P, 512], F32, name=f"gain_b{q}") for q in TPQ}
+        atom_oc = [keep.tile([P, 1024], U8, name=f"atom_oc{g}", align_bytes=64) for g in range(N_GROUPS)]
+        atom_os = [keep.tile([P, 512], U8, name=f"atom_os{g}", align_bytes=64) for g in range(N_GROUPS)]
+        gain_row = {quad: keep.tile([P, 512], F32, name=f"gain_row{quad}") for quad in COLUMN_QUADS}
         foot_c = keep.tile([P, 2 * REC], U8, name="foot_c", align_bytes=64)
         foot_s = keep.tile([P, REC], U8, name="foot_s", align_bytes=64)
         ident = keep.tile([P, P], F32, name="ident")
-        rows16 = keep.tile([P, P], BF16, name="rows16")
-        rows32 = keep.tile([P, P], F32, name="rows32")
-        gain = keep.tile([P, n_rt], F32, name="gain")
-        warm = keep.tile([P, 1], F32, name="warm")
-        filt_q = [[keep.tile([P, 512], U32, name=f"filt_q{g}{c}", align_bytes=64) for c in range(n_c)] for g in range(n_g)]
-        filt_s = [[keep.tile([P, 512], U8, name=f"filt_s{g}{c}", align_bytes=64) for c in range(n_c)] for g in range(n_g)]
-        occ_q = [[keep.tile([P, 512], U32, name=f"occ_q{c}{h}", align_bytes=64) for h in range(2)] for c in range(n_c)]
-        occ_s = [[keep.tile([P, 512], U8, name=f"occ_s{c}{h}", align_bytes=64) for h in range(2)] for c in range(n_c)]
-        e_q = [[keep.tile([P, 512], U32, name=f"e_q{g}{h}", align_bytes=64) for h in range(2)] for g in range(n_g)]
-        e_s = [[keep.tile([P, 512], U8, name=f"e_s{g}{h}", align_bytes=64) for h in range(2)] for g in range(n_g)]
-        f_q = [keep.tile([P, 512], U32, name=f"f_q{k}", align_bytes=64) for k in range(n_rt // 2)]
-        f_s = [keep.tile([P, 512], U8, name=f"f_s{k}", align_bytes=64) for k in range(n_rt // 2)]
-        filt_x = [[keep.tile([P, 2, RAW], BF16, name=f"filt_x{g}{jp}") for jp in range(2)] for g in range(n_g)]
-        occ_x = [[outs.tile([P, 2048], BF16, name=f"occ_x{c}{h}", tag="io") for h in range(2)] for c in range(n_c)]
-        occ_k = [[None, None] for c in range(n_c)]
+        recv16 = keep.tile([P, P], BF16, name="recv16")
+        recv32 = keep.tile([P, P], F32, name="recv32")
+        gain = keep.tile([P, N_TILES], F32, name="gain")
+        exp_seed = keep.tile([P, 1], F32, name="exp_seed")
 
-        nc.vector.memset(rows16[:], 0.0)
+        def codes_and_scales(name, rows, columns):
+            codes = [[keep.tile([P, 512], U32, name=f"{name}_q{r}{c}", align_bytes=64) for c in range(columns)] for r in range(rows)]
+            scales = [[keep.tile([P, 512], U8, name=f"{name}_s{r}{c}", align_bytes=64) for c in range(columns)] for r in range(rows)]
+            return codes, scales
+
+        filt_q, filt_s = codes_and_scales("filt", N_GROUPS, N_CHUNKS)
+        occ_q, occ_s = codes_and_scales("occ", N_CHUNKS, 2)
+        e_q, e_s = codes_and_scales("e", N_GROUPS, 2)
+        f_q = [keep.tile([P, 512], U32, name=f"f_q{k}", align_bytes=64) for k in range(N_TILES // 2)]
+        f_s = [keep.tile([P, 512], U8, name=f"f_s{k}", align_bytes=64) for k in range(N_TILES // 2)]
+        filt_raw = [[keep.tile([P, 2, RAW], BF16, name=f"filt_raw{g}{jp}") for jp in range(2)] for g in range(N_GROUPS)]
+        occ_raw = [[ring.tile([P, 2048], BF16, name=f"occ_raw{c}{h}", tag="ring") for h in range(2)] for c in range(N_CHUNKS)]
+
         nc.vector.memset(atom_s[:].bitcast(I32), 0)
         nc.vector.memset(foot_s[:].bitcast(I32), 0)
-        nc.vector.memset(warm[:], 0.0)
         nc.vector.memset(ident[:], 0.0)
-        nc.gpsimd.affine_select(
-            out=ident[:], in_=ident[:], pattern=[[-1, P]], compare_op=mybir.AluOpType.not_equal, fill=1.0, base=0, channel_multiplier=1
-        )
+        nc.vector.memset(recv16[:], 0.0)
+        nc.vector.memset(exp_seed[:], 0.0)
 
         def load_filt(g, jp):
-            src = filt[512 * g : 512 * (g + 1), :].rearrange("(m j) k -> m j k", j=4)
-            nc.sync.dma_start(out=filt_x[g][jp][:], in_=src[:, 2 * jp : 2 * jp + 2, :])
+            rows = filt[512 * g : 512 * (g + 1), :].rearrange("(m j) k -> m j k", j=4)
+            nc.sync.dma_start(out=filt_raw[g][jp][:], in_=rows[:, 2 * jp : 2 * jp + 2, :])
 
         def load_occ(c, h):
-            src = occ[512 * c : 512 * (c + 1), :].rearrange("(p j) l -> p j l", j=4)
-            nc.sync.dma_start(out=occ_x[c][h][:].rearrange("p (j l) -> p j l", j=4), in_=src[:, :, 512 * h : 512 * (h + 1)])
+            rows = occ[512 * c : 512 * (c + 1), :].rearrange("(p j) l -> p j l", j=4)
+            nc.sync.dma_start(
+                out=occ_raw[c][h][:].rearrange("p (j l) -> p j l", j=4), in_=rows[:, :, 512 * h : 512 * (h + 1)]
+            )
+
+        def load_scales(engine, plane, scales, quarter):
+            engine.dma_start(
+                out=plane[32 * quarter : 32 * quarter + 4, :].bitcast(I32),
+                in_=scales[0][4 * quarter : 4 * quarter + 4, :].bitcast(I32),
+            )
 
         load_filt(0, 0)
         nc.sync.dma_start(out=atom_c[:].bitcast(I32), in_=atom_words[0].bitcast(I32))
         nc.sync.dma_start(out=foot_c[:].bitcast(I32), in_=foot_words[0].bitcast(I32))
-        nc.gpsimd.dma_start(out=rows16[0:n_rt, :], in_=recv.rearrange("(c n) -> c n", n=P))
-        for q in range(4):
-            nc.scalar.dma_start(
-                out=atom_s[32 * q : 32 * q + 4, :].bitcast(I32), in_=atom_scales[0][4 * q : 4 * q + 4, :].bitcast(I32)
-            )
-        for q in range(4):
-            (nc.scalar if q < 1 else nc.sync if q < 3 else nc.gpsimd).dma_start(
-                out=foot_s[32 * q : 32 * q + 4, :].bitcast(I32), in_=foot_scales[0][4 * q : 4 * q + 4, :].bitcast(I32)
-            )
-        nc.scalar.activation(warm[:], warm[:], EXP)
-        for step in LOADS:
-            if step[0] == "f":
-                load_filt(int(step[1]), int(step[2]))
+        for quarter in range(4):
+            load_scales(nc.scalar, atom_s, atom_scales, quarter)
+        load_scales(nc.scalar, foot_s, foot_scales, 0)
+        nc.gpsimd.affine_select(
+            out=ident[:], in_=ident[:], pattern=[[-1, P]], compare_op=NOT_EQUAL, fill=1.0, base=0, channel_multiplier=1
+        )
+        nc.gpsimd.dma_start(out=recv16[0:N_TILES, :], in_=recv.rearrange("(c n) -> c n", n=P))
+        load_scales(nc.gpsimd, foot_s, foot_scales, 3)
+        nc.scalar.activation(exp_seed[:], exp_seed[:], EXP)
+        load_filt(0, 1)
+        load_scales(nc.sync, foot_s, foot_scales, 1)
+        load_scales(nc.sync, foot_s, foot_scales, 2)
+        for name, first, second in LATER_LOADS:
+            if name == "filt":
+                load_filt(first, second)
             else:
-                load_occ(int(step[1]), int(step[2]))
+                load_occ(first, second)
 
-        nc.vector.tensor_copy(out=rows32[:], in_=rows16[:])
-
-        ops = {}
-
-        def op(name, needs, fn):
-            ops[name] = (needs, fn)
+        nc.vector.tensor_copy(out=recv32[:], in_=recv16[:])
 
         banks = {}
 
-        def new_bank(key):
-            bank = psum.tile([P, BANK], F32, name="bank")
-            banks[key] = bank
-            return bank
+        def new_bank(step):
+            banks[step] = psum.tile([P, BANK], F32, name="bank")
+            return banks[step]
 
-        def gain_t():
-            nc.tensor.transpose(new_bank("gain")[:, 0:P], rows32[:], ident[:])
+        def copy_on(engine, dst, src):
+            if engine == "V":
+                nc.vector.tensor_copy(out=dst, in_=src)
+            else:
+                nc.scalar.copy(dst, src)
 
-        def gain_s():
-            nc.scalar.activation(gain[:], banks["gain"][:, 0:n_rt], EXP)
+        def quantize(codes, scales, values):
+            nc.vector.quantize_mx(out=codes[:].bitcast(FP8X4), scales=scales[:], in_=values[:])
 
-        op("gt", [], gain_t)
-        op("gs", ["gt"], gain_s)
+        def recv_t():
+            nc.tensor.transpose(new_bank("recv")[:, 0:P], recv32[:], ident[:])
 
-        f_nat = {}
-        f_k = {}
+        def make_gain():
+            nc.scalar.activation(gain[:], banks["recv"][:, 0:N_TILES], EXP)
 
-        def f1(rt, g):
+        def gain_t(quad):
+            bank = new_bank(("gain", quad))
+            for i in range(4):
+                tile = 4 * quad + i
+                nc.tensor.transpose(bank[:, P * i : P * (i + 1)], gain[:, tile : tile + 1].to_broadcast([P, P]), ident[:])
+
+        def make_gain_row(quad):
+            nc.scalar.copy(gain_row[quad][:], banks["gain", quad][:])
+
+        natural = {}
+        f_values = {}
+
+        def row_mm(tile, g):
             nc.tensor.matmul_mx(
-                out=new_bank(("f", rt, g))[:],
-                lhsT=foot_c[:, 256 * rt : 256 * (rt + 1)].bitcast(FP4X4),
-                lhsT_scale=foot_s[:, P * rt : P * (rt + 1)],
+                out=new_bank(("row", tile, g))[:],
+                lhsT=foot_c[:, 256 * tile : 256 * (tile + 1)].bitcast(FP4X4),
+                lhsT_scale=foot_s[:, P * tile : P * (tile + 1)],
                 rhs=atom_c[:, 1024 * g : 1024 * (g + 1)].bitcast(FP4X4),
                 rhs_scale=atom_s[:, 512 * g : 512 * (g + 1)],
                 start=True,
                 stop=True,
             )
 
-        def fd(rt, g, engine):
-            if rt not in f_nat:
-                f_nat[rt] = work.tile([P, TEX], BF16, name="nat", bufs=8)
-            dst = f_nat[rt][:, 512 * g : 512 * (g + 1)].rearrange("p (u b i e) -> p u b i e", u=2, i=4, e=2)
-            src = banks["f", rt, g][:].rearrange("p (b u e i) -> p u b i e", u=2, i=4, e=2)
-            parts = [(dst, src)] if not SPLIT_D else [(dst[:, u], src[:, u]) for u in range(2)]
-            for d, s in parts:
+        def row_gain(engine, tile, g):
+            if tile not in natural:
+                natural[tile] = work.tile([P, TEX], BF16, name="natural", bufs=8)
+            dst = natural[tile][:, 512 * g : 512 * (g + 1)].rearrange("p (u b i v) -> p u b i v", u=2, i=4, v=2)
+            src = banks["row", tile, g][:].rearrange("p (b u v i) -> p u b i v", u=2, i=4, v=2)
+            for u in range(2):
                 if engine == "V":
-                    nc.vector.tensor_scalar_mul(d, s, gain[:, rt : rt + 1])
+                    nc.vector.tensor_scalar_mul(dst[:, u], src[:, u], gain[:, tile : tile + 1])
                 else:
-                    nc.scalar.activation(d, s, COPY, scale=gain[:, rt : rt + 1])
+                    nc.scalar.activation(dst[:, u], src[:, u], COPY, scale=gain[:, tile : tile + 1])
 
-        def ft(rt):
-            words = f_nat[rt][:].bitcast(F32)
-            bank = new_bank(("t", rt))
+        def row_t(tile):
+            words = natural[tile][:].bitcast(F32)
+            bank = new_bank(("row_t", tile))
             for b in range(4):
                 nc.tensor.transpose(bank[:, P * b : P * (b + 1)], words[:, P * b : P * (b + 1)], ident[:])
 
-        def fw(rt, engine):
-            k, i = rt // 2, rt % 2
-            if k not in f_k:
-                f_k[k] = work.tile([P, 2048], BF16, name="f_kt", bufs=4, align_bytes=64)
-            dst = f_k[k][:, 1024 * i : 1024 * (i + 1)].bitcast(F32).rearrange("p (g r u) -> p g r u", g=2, u=2)
-            src = banks["t", rt][:].rearrange("p (g u r) -> p g r u", g=2, u=2)
-            if engine == "V":
-                nc.vector.tensor_copy(out=dst, in_=src)
-            else:
-                nc.scalar.copy(dst, src)
+        def row_pack(engine, tile):
+            pair, i = divmod(tile, 2)
+            if pair not in f_values:
+                f_values[pair] = work.tile([P, 2048], BF16, name="f_values", bufs=4, align_bytes=64)
+            dst = f_values[pair][:, 1024 * i : 1024 * (i + 1)].bitcast(F32).rearrange("p (g r u) -> p g r u", g=2, u=2)
+            copy_on(engine, dst, banks["row_t", tile][:].rearrange("p (g u r) -> p g r u", g=2, u=2))
 
-        def fq(k):
-            nc.vector.quantize_mx(out=f_q[k][:].bitcast(FP8X4), scales=f_s[k][:], in_=f_k[k][:])
+        def row_q(pair):
+            quantize(f_q[pair], f_s[pair], f_values[pair])
 
-        w_t = {}
+        w_gained = {}
 
-        def atoms(g):
+        def atom_order(g):
             nc.vector.tensor_copy(
-                out=atom_pc[g][:].bitcast(I32).rearrange("p (t b w) -> p t b w", t=4, w=2),
+                out=atom_oc[g][:].bitcast(I32).rearrange("p (t b w) -> p t b w", t=4, w=2),
                 in_=atom_c[:, 1024 * g : 1024 * (g + 1)].bitcast(I32).rearrange("p (b t w) -> p t b w", t=4, w=2),
             )
             nc.vector.tensor_copy(
-                out=atom_ps[g][:].bitcast(I32).rearrange("p (t b) -> p t b", t=4),
+                out=atom_os[g][:].bitcast(I32).rearrange("p (t b) -> p t b", t=4),
                 in_=atom_s[:, 512 * g : 512 * (g + 1)].bitcast(I32).rearrange("p (b t) -> p t b", t=4),
             )
 
-        def gain_cols(q):
-            bank = new_bank(("g", q))
-            for i in range(4):
-                rt = 4 * q + i
-                nc.tensor.transpose(bank[:, P * i : P * (i + 1)], gain[:, rt : rt + 1].to_broadcast([P, P]), ident[:])
-
-        def gains(q):
-            nc.scalar.copy(gain_b[q][:], banks["g", q][:])
-
-        def u1(q, g, t):
+        def col_mm(quad, g, t):
             nc.tensor.matmul_mx(
-                out=new_bank(("u", q, g, t))[:],
-                lhsT=atom_pc[g][:, 256 * t : 256 * (t + 1)].bitcast(FP4X4),
-                lhsT_scale=atom_ps[g][:, P * t : P * (t + 1)],
-                rhs=foot_c[:, 1024 * q : 1024 * (q + 1)].bitcast(FP4X4),
-                rhs_scale=foot_s[:, 512 * q : 512 * (q + 1)],
+                out=new_bank(("col", quad, g, t))[:],
+                lhsT=atom_oc[g][:, 256 * t : 256 * (t + 1)].bitcast(FP4X4),
+                lhsT_scale=atom_os[g][:, P * t : P * (t + 1)],
+                rhs=foot_c[:, 1024 * quad : 1024 * (quad + 1)].bitcast(FP4X4),
+                rhs_scale=foot_s[:, 512 * quad : 512 * (quad + 1)],
                 start=True,
                 stop=True,
             )
 
-        def yd(q, g, t):
-            if (q, g) not in w_t:
-                w_t[q, g] = work.tile([P, 4, 512], BF16, name="w_t", bufs=2)
-            nc.vector.tensor_tensor(out=w_t[q, g][:, t, :], in0=banks["u", q, g, t][:], in1=gain_b[q][:], op=mybir.AluOpType.mult)
+        def col_gain(quad, g, t):
+            if (quad, g) not in w_gained:
+                w_gained[quad, g] = work.tile([P, 4, 512], BF16, name="w_gained", bufs=2)
+            nc.vector.tensor_tensor(
+                out=w_gained[quad, g][:, t, :], in0=banks["col", quad, g, t][:], in1=gain_row[quad][:], op=MULT
+            )
 
-        def fi(q, g, engine):
-            f_k[q, g] = work.tile([P, 2048], BF16, name="f_kt", bufs=4, align_bytes=64)
-            dst = f_k[q, g][:].rearrange("p (c i t) -> p c t i", i=4, t=4)
-            src = w_t[q, g][:].rearrange("p t (c i) -> p c t i", i=4)
-            if engine == "V":
-                nc.vector.tensor_copy(out=dst, in_=src)
-            else:
-                nc.scalar.copy(dst, src)
+        def interleave(engine, dst, src):
+            copy_on(
+                engine,
+                dst[:].rearrange("p (c i t) -> p c t i", i=4, t=4),
+                src.rearrange("p (t c i) -> p c t i", t=4, i=4),
+            )
 
-        def tq(q, g):
-            k = 2 * q + g
-            nc.vector.quantize_mx(out=f_q[k][:].bitcast(FP8X4), scales=f_s[k][:], in_=f_k[q, g][:])
+        def col_pack(engine, quad, g):
+            f_values[quad, g] = work.tile([P, 2048], BF16, name="f_values", bufs=4, align_bytes=64)
+            interleave(engine, f_values[quad, g], w_gained[quad, g][:].rearrange("p t n -> p (t n)"))
 
-        filt_k = {}
+        def col_q(quad, g):
+            quantize(f_q[2 * quad + g], f_s[2 * quad + g], f_values[quad, g])
 
-        def at(g, jp, c):
-            words = filt_x[g][jp][:].rearrange("p j k -> p (j k)").bitcast(F32)
-            bank = new_bank(("a", g, jp, c))
+        filt_values = {}
+        occ_values = {}
+
+        def filt_t(g, jp, c):
+            words = filt_raw[g][jp][:].rearrange("p j k -> p (j k)").bitcast(F32)
+            bank = new_bank(("filt", g, jp, c))
             for j in range(2):
                 for u in range(2):
-                    w0 = 768 * j + 256 * c
+                    first = (RAW // 2) * j + 256 * c
                     b = 2 * j + u
-                    nc.tensor.transpose(bank[:, P * b : P * (b + 1)], words[:, w0 + u : w0 + 256 : 2], ident[:])
+                    nc.tensor.transpose(bank[:, P * b : P * (b + 1)], words[:, first + u : first + 256 : 2], ident[:])
 
-        def ac(g, jp, c, engine):
-            if (g, c) not in filt_k:
-                filt_k[g, c] = work.tile([P, 2048], BF16, name="filt_k", bufs=5, align_bytes=64)
-            dst = filt_k[g, c][:].bitcast(F32).rearrange("p (t b x) -> p t b x", t=4, x=8)[:, :, :, 4 * jp : 4 * jp + 4]
-            src = banks["a", g, jp, c][:].rearrange("p (x b t) -> p t b x", t=4, x=4)
-            if engine == "V":
-                nc.vector.tensor_copy(out=dst, in_=src)
-            else:
-                nc.scalar.copy(dst, src)
+        def filt_pack(engine, g, jp, c):
+            if (g, c) not in filt_values:
+                filt_values[g, c] = work.tile([P, 2048], BF16, name="filt_values", bufs=5, align_bytes=64)
+            dst = filt_values[g, c][:].bitcast(F32).rearrange("p (t b x) -> p t b x", t=4, x=8)[:, :, :, 4 * jp : 4 * jp + 4]
+            copy_on(engine, dst, banks["filt", g, jp, c][:].rearrange("p (x b t) -> p t b x", t=4, x=4))
 
-        def aq(g, c):
-            nc.vector.quantize_mx(out=filt_q[g][c][:].bitcast(FP8X4), scales=filt_s[g][c][:], in_=filt_k[g, c][:])
+        def filt_quant(g, c):
+            quantize(filt_q[g][c], filt_s[g][c], filt_values[g, c])
 
-        def bi(c, h, engine):
-            occ_k[c][h] = work.tile([P, 2048], BF16, name="occ_kt", bufs=4, align_bytes=64)
-            dst = occ_k[c][h][:].rearrange("p (c i j) -> p c j i", i=4, j=4)
-            src = occ_x[c][h][:].rearrange("p (j c i) -> p c j i", j=4, i=4)
-            if engine == "V":
-                nc.vector.tensor_copy(out=dst, in_=src)
-            else:
-                nc.scalar.copy(dst, src)
+        def occ_pack(engine, c, h):
+            occ_values[c, h] = work.tile([P, 2048], BF16, name="occ_values", bufs=4, align_bytes=64)
+            interleave(engine, occ_values[c, h], occ_raw[c][h][:])
 
-        def bq(c, h):
-            nc.vector.quantize_mx(out=occ_q[c][h][:].bitcast(FP8X4), scales=occ_s[c][h][:], in_=occ_k[c][h][:])
+        def occ_quant(c, h):
+            quantize(occ_q[c][h], occ_s[c][h], occ_values[c, h])
 
-        e_k = {}
+        e_values = {}
 
-        def s2(g, h, i):
-            bank = new_bank(("s", g, h, i))
+        def map_mm(g, h, i):
+            bank = new_bank(("map", g, h, i))
             for t in range(4):
-                for c in range(n_c):
+                for c in range(N_CHUNKS):
                     nc.tensor.matmul_mx(
                         out=bank[:, P * t : P * (t + 1)],
                         lhsT=filt_q[g][c][:, P * t : P * (t + 1)].bitcast(FP8X4),
@@ -292,131 +305,117 @@ def tile_exponential_shadow_visibility_s12_kernel(
                         rhs=occ_q[c][h][:, P * i : P * (i + 1)].bitcast(FP8X4),
                         rhs_scale=occ_s[c][h][:, P * i : P * (i + 1)],
                         start=(c == 0),
-                        stop=(c == n_c - 1),
+                        stop=(c == N_CHUNKS - 1),
                     )
 
-        def ec(g, h, i, engine):
-            if (g, h) not in e_k:
-                e_k[g, h] = work.tile([P, 2048], BF16, name="e_kt", bufs=4, align_bytes=64)
-            dst = e_k[g, h][:, 512 * i : 512 * (i + 1)].rearrange("p (n t) -> p n t", t=4)
-            src = banks["s", g, h, i][:].rearrange("p (t n) -> p n t", t=4)
-            if engine == "V":
-                nc.vector.tensor_copy(out=dst, in_=src)
-            else:
-                nc.scalar.copy(dst, src)
+        def map_pack(engine, g, h, i):
+            if (g, h) not in e_values:
+                e_values[g, h] = work.tile([P, 2048], BF16, name="e_values", bufs=4, align_bytes=64)
+            dst = e_values[g, h][:, 512 * i : 512 * (i + 1)].rearrange("p (n t) -> p n t", t=4)
+            copy_on(engine, dst, banks["map", g, h, i][:].rearrange("p (t n) -> p n t", t=4))
 
-        def eq(g, h):
-            nc.vector.quantize_mx(out=e_q[g][h][:].bitcast(FP8X4), scales=e_s[g][h][:], in_=e_k[g, h][:])
+        def map_quant(g, h):
+            quantize(e_q[g][h], e_s[g][h], e_values[g, h])
 
-        out_t = {}
+        out_tiles = {}
+        halves_done = {}
 
-        def s3(rt, h):
-            k, i = rt // 2, rt % 2
-            bank = new_bank(("o", rt, h))
-            for g in range(n_g):
-                if rt // 4 in TPQ:
-                    k, j = 2 * (rt // 4) + g, rt % 4
+        def out_mm(tile, h):
+            bank = new_bank(("out", tile, h))
+            for g in range(N_GROUPS):
+                if tile // 4 in COLUMN_QUADS:
+                    k, j = 2 * (tile // 4) + g, tile % 4
                 else:
-                    k, j = rt // 2, 2 * i + g
-                cols = slice(P * j, P * (j + 1))
+                    k, j = tile // 2, 2 * (tile % 2) + g
+                columns = slice(P * j, P * (j + 1))
                 nc.tensor.matmul_mx(
                     out=bank[:],
-                    lhsT=f_q[k][:, cols].bitcast(FP8X4),
-                    lhsT_scale=f_s[k][:, cols],
+                    lhsT=f_q[k][:, columns].bitcast(FP8X4),
+                    lhsT_scale=f_s[k][:, columns],
                     rhs=e_q[g][h][:].bitcast(FP8X4),
                     rhs_scale=e_s[g][h][:],
                     start=(g == 0),
-                    stop=(g == n_g - 1),
+                    stop=(g == N_GROUPS - 1),
                 )
 
-        def od(rt, h, engine):
-            if (rt // 2, h) not in out_t:
-                out_t[rt // 2, h] = outs.tile([P, 1024], F32, name="out_t", tag="io")
-            dst = out_t[rt // 2, h][:, 512 * (rt % 2) : 512 * (rt % 2 + 1)]
+        def store(tile, h):
+            halves_done[tile] = halves_done.get(tile, 0) + 1
+            if tile == LAST_TILE:
+                columns = slice(512 * h, 512 * (h + 1))
+                nc.sync.dma_start(out=out[P * tile : P * (tile + 1), columns], in_=out_tiles[tile][:, columns])
+            elif halves_done[tile] == 2:
+                nc.sync.dma_start(out=out[P * tile : P * (tile + 1), :], in_=out_tiles[tile][:])
+
+        def out_copy(engine, tile, h):
+            if tile not in out_tiles:
+                out_tiles[tile] = ring.tile([P, FRM], F32, name="out_tile", tag="ring")
+            dst = out_tiles[tile][:, 512 * h : 512 * (h + 1)]
             if engine == "V":
-                nc.vector.tensor_scalar_min(dst, banks["o", rt, h][:], 1.0)
-                nc.sync.dma_start(out=out[P * rt : P * (rt + 1), 512 * h : 512 * (h + 1)], in_=dst)
+                nc.vector.tensor_scalar_min(dst, banks["out", tile, h][:], 1.0)
+                store(tile, h)
             else:
-                nc.scalar.copy(dst, banks["o", rt, h][:])
+                nc.scalar.copy(dst, banks["out", tile, h][:])
 
-        def om(rt, h):
-            dst = out_t[rt // 2, h][:, 512 * (rt % 2) : 512 * (rt % 2 + 1)]
+        def out_min(tile, h):
+            dst = out_tiles[tile][:, 512 * h : 512 * (h + 1)]
             nc.vector.tensor_scalar_min(dst, dst, 1.0)
-            nc.sync.dma_start(out=out[P * rt : P * (rt + 1), 512 * h : 512 * (h + 1)], in_=dst)
+            store(tile, h)
 
-        def run(token):
-            a = token.split(".")
-            n = [int(x) for x in a[1:] if x not in ("V", "S")]
-            e = a[len(a) - 1]
-            k = a[0]
-            if k == "gt":
-                return [], gain_t
-            if k == "gs":
-                return ["gt"], gain_s
-            if k == "F":
-                return [], lambda: f1(*n)
-            if k == "D":
-                return ["gs", "F.%d.%d" % (n[0], n[1])], lambda: fd(n[0], n[1], e)
-            if k == "T":
-                return ["D.%d.0" % n[0], "D.%d.1" % n[0]], lambda: ft(*n)
-            if k == "W":
-                return ["T.%d" % n[0]], lambda: fw(n[0], e)
-            if k == "FQ":
-                return ["W.%d" % (2 * n[0]), "W.%d" % (2 * n[0] + 1)], lambda: fq(*n)
-            if k == "AT":
-                return [], lambda: at(*n)
-            if k == "A":
-                return ["AT.%d.%d.%d" % (n[0], n[1], n[2])], lambda: ac(n[0], n[1], n[2], e)
-            if k == "AQ":
-                return ["A.%d.%d.%d" % (n[0], jp, n[1]) for jp in range(2)], lambda: aq(*n)
-            if k == "B":
-                return [], lambda: bi(n[0], n[1], e)
-            if k == "BQ":
-                return ["B.%d.%d" % (n[0], n[1])], lambda: bq(*n)
-            if k == "S2":
-                return ["AQ.%d.%d" % (n[0], c) for c in range(3)] + ["BQ.%d.%d" % (c, n[1]) for c in range(3)], lambda: s2(*n)
-            if k == "C":
-                return ["S2.%d.%d.%d" % (n[0], n[1], n[2])], lambda: ec(n[0], n[1], n[2], e)
-            if k == "EQ":
-                return ["C.%d.%d.%d" % (n[0], n[1], i) for i in range(4)], lambda: eq(*n)
-            if k == "S3":
-                fd_ = ["TQ.%d.%d" % (n[0] // 4, g) for g in range(2)] if n[0] // 4 in TPQ else ["FQ.%d" % (n[0] // 2)]
-                return fd_ + ["EQ.%d.%d" % (g, n[1]) for g in range(2)], lambda: s3(*n)
-            if k == "O":
-                return ["S3.%d.%d" % (n[0], n[1])], lambda: od(n[0], n[1], e)
-            if k == "P":
-                return [], lambda: atoms(*n)
-            if k == "GB":
-                return ["gs"], lambda: gain_cols(*n)
-            if k == "X":
-                return ["GB.%d" % n[0]], lambda: gains(*n)
-            if k == "U":
-                return ["P.%d" % n[1]], lambda: u1(*n)
-            if k == "Y":
-                return ["X.%d" % n[0], "U.%d.%d.%d" % (n[0], n[1], n[2])], lambda: yd(*n)
-            if k == "I":
-                return ["Y.%d.%d.%d" % (n[0], n[1], t) for t in range(4)], lambda: fi(n[0], n[1], e)
-            if k == "TQ":
-                return ["I.%d.%d" % (n[0], n[1])], lambda: tq(*n)
-            if k == "M":
-                return ["O.%d.%d" % (n[0], n[1])], lambda: om(*n)
-            raise ValueError(token)
+        def f_ready(tile):
+            if tile // 4 in COLUMN_QUADS:
+                return [("ColQ", tile // 4, g) for g in range(N_GROUPS)]
+            return [("RowQ", tile // 2)]
 
-        queues = [T_ORDER.split(), V_ORDER.split(), S_ORDER.split()]
-        names = ["", ".V", ".S"]
-        done = set()
-        at_q = [0, 0, 0]
-        total = sum([len(q) for q in queues])
-        while len(done) < total:
-            before = len(done)
-            for j in range(3):
-                while at_q[j] < len(queues[j]):
-                    token = queues[j][at_q[j]]
-                    needs, fn = run(token + names[j])
-                    if not all([x in done for x in needs]):
+        kinds = {
+            "RecvT": (lambda: [], recv_t, False),
+            "Gain": (lambda: [("RecvT",)], make_gain, False),
+            "GainT": (lambda quad: [("Gain",)], gain_t, False),
+            "GainRow": (lambda quad: [("GainT", quad)], make_gain_row, False),
+            "RowMM": (lambda tile, g: [], row_mm, False),
+            "RowGain": (lambda tile, g: [("Gain",), ("RowMM", tile, g)], row_gain, True),
+            "RowT": (lambda tile: [("RowGain", tile, g) for g in range(N_GROUPS)], row_t, False),
+            "RowPack": (lambda tile: [("RowT", tile)], row_pack, True),
+            "RowQ": (lambda pair: [("RowPack", 2 * pair + i) for i in range(2)], row_q, False),
+            "AtomOrder": (lambda g: [], atom_order, False),
+            "ColMM": (lambda quad, g, t: [("AtomOrder", g)], col_mm, False),
+            "ColGain": (lambda quad, g, t: [("GainRow", quad), ("ColMM", quad, g, t)], col_gain, False),
+            "ColPack": (lambda quad, g: [("ColGain", quad, g, t) for t in range(4)], col_pack, True),
+            "ColQ": (lambda quad, g: [("ColPack", quad, g)], col_q, False),
+            "FiltT": (lambda g, jp, c: [], filt_t, False),
+            "FiltPack": (lambda g, jp, c: [("FiltT", g, jp, c)], filt_pack, True),
+            "FiltQ": (lambda g, c: [("FiltPack", g, jp, c) for jp in range(2)], filt_quant, False),
+            "OccPack": (lambda c, h: [], occ_pack, True),
+            "OccQ": (lambda c, h: [("OccPack", c, h)], occ_quant, False),
+            "MapMM": (
+                lambda g, h, i: [("FiltQ", g, c) for c in range(N_CHUNKS)] + [("OccQ", c, h) for c in range(N_CHUNKS)],
+                map_mm,
+                False,
+            ),
+            "MapPack": (lambda g, h, i: [("MapMM", g, h, i)], map_pack, True),
+            "MapQ": (lambda g, h: [("MapPack", g, h, i) for i in range(4)], map_quant, False),
+            "OutMM": (lambda tile, h: f_ready(tile) + [("MapQ", g, h) for g in range(N_GROUPS)], out_mm, False),
+            "OutCopy": (lambda tile, h: [("OutMM", tile, h)], out_copy, True),
+            "OutMin": (lambda tile, h: [("OutCopy", tile, h)], out_min, False),
+        }
+
+        def parse(table):
+            return [(word.split(".")[0],) + tuple([int(n) for n in word.split(".")[1:]]) for word in table.split()]
+
+        waiting = {"T": parse(TENSOR_ORDER), "V": parse(VECTOR_ORDER), "S": parse(SCALAR_ORDER)}
+        called = set()
+        while any(waiting.values()):
+            before = len(called)
+            for engine, steps in waiting.items():
+                while steps:
+                    step = steps[0]
+                    needs, function, takes_engine = kinds[step[0]]
+                    if not all([need in called for need in needs(*step[1:])]):
                         break
-                    fn()
-                    done.add(token)
-                    at_q[j] += 1
-            if len(done) == before:
-                raise ValueError([q[i] for q, i in zip(queues, at_q) if i < len(q)])
+                    if takes_engine:
+                        function(engine, *step[1:])
+                    else:
+                        function(*step[1:])
+                    called.add(step)
+                    steps.remove(step)
+            if len(called) == before:
+                raise ValueError("the tables' orders contradict the steps' needs")

from contextlib import ExitStack

import concourse.mybir as mybir

REC, CODES, TEX, RAW, FRM = 2048, 512, 1024, 1536, 1024

FLOPS = 2 * (REC * TEX * CODES + TEX * FRM * RAW + REC * FRM * TEX)

F32 = mybir.dt.float32
BF16 = mybir.dt.bfloat16
U32 = mybir.dt.uint32
I32 = mybir.dt.int32
U8 = mybir.dt.uint8
FP8X4 = mybir.dt.float8_e4m3fn_x4
FP4X4 = mybir.dt.float4_e2m1fn_x4
COPY = mybir.ActivationFunctionType.Copy
EXP = mybir.ActivationFunctionType.Exp
MULT = mybir.AluOpType.mult
NOT_EQUAL = mybir.AluOpType.not_equal

P = 128
BANK = 512
N_TILES = REC // P
N_GROUPS = TEX // 512
N_CHUNKS = RAW // 512
LAST_TILE = N_TILES - 1

COLUMN_QUADS = (0, 2)

LATER_LOADS = (("occ", 0, 0), ("occ", 1, 0), ("occ", 2, 0), ("filt", 1, 0), ("filt", 1, 1), ("occ", 0, 1), ("occ", 1, 1), ("occ", 2, 1))

TENSOR_ORDER = """
FiltT.0.0.0 FiltT.0.0.1 FiltT.0.0.2 RecvT GainT.0 RowMM.4.0 RowMM.4.1 RowMM.5.0 ColMM.0.0.0 RowMM.5.1
RowMM.6.0 FiltT.0.1.0 GainT.2 FiltT.0.1.1 FiltT.0.1.2 ColMM.0.0.1 RowMM.6.1 FiltT.1.0.0 FiltT.1.0.1
FiltT.1.0.2 ColMM.0.0.2 RowMM.7.0 RowMM.7.1 ColMM.0.0.3 ColMM.0.1.0 RowT.4 FiltT.1.1.0 FiltT.1.1.1 FiltT.1.1.2
RowT.5 ColMM.0.1.1 MapMM.0.0.0 MapMM.0.0.1 MapMM.0.0.2 MapMM.0.0.3 MapMM.1.0.0 ColMM.0.1.2 MapMM.1.0.1
ColMM.0.1.3 MapMM.1.0.2 MapMM.1.0.3 ColMM.2.0.0 ColMM.2.0.1 MapMM.0.1.0 ColMM.2.0.2 MapMM.0.1.1 MapMM.0.1.2
ColMM.2.0.3 MapMM.0.1.3 ColMM.2.1.0 MapMM.1.1.0 MapMM.1.1.1 RowMM.12.0 ColMM.2.1.1 MapMM.1.1.2 MapMM.1.1.3
ColMM.2.1.2 ColMM.2.1.3 OutMM.0.0 RowT.6 RowT.7 RowMM.12.1 RowMM.13.0 OutMM.0.1 OutMM.1.0 OutMM.1.1 OutMM.2.0
OutMM.2.1 OutMM.3.0 OutMM.3.1 OutMM.4.0 OutMM.4.1 RowMM.13.1 RowMM.14.0 RowMM.14.1 OutMM.5.0 OutMM.5.1
RowMM.15.0 RowMM.15.1 OutMM.6.0 OutMM.6.1 OutMM.7.0 OutMM.7.1 OutMM.8.0 OutMM.8.1 RowT.12 RowT.13 RowT.14
RowT.15 OutMM.9.0 OutMM.9.1 OutMM.10.0 OutMM.10.1 OutMM.11.0 OutMM.11.1 OutMM.12.0 OutMM.12.1 OutMM.13.0
OutMM.13.1 OutMM.14.0 OutMM.14.1 OutMM.15.0 OutMM.15.1
"""
VECTOR_ORDER = """
FiltPack.0.0.0 AtomOrder.0 AtomOrder.1 FiltPack.0.0.1 FiltPack.0.0.2 OccPack.0.0 OccPack.1.0 ColGain.0.0.0
OccQ.0.0 OccPack.2.0 FiltQ.0.0 ColGain.0.0.1 FiltQ.0.1 FiltQ.0.2 ColGain.0.0.2 OccQ.1.0 OccQ.2.0 ColGain.0.0.3
ColGain.0.1.0 ColGain.0.1.1 FiltQ.1.0 FiltQ.1.1 FiltQ.1.2 OccPack.0.1 OccPack.1.1 OccQ.0.1 OccQ.1.1 OccQ.2.1
ColGain.0.1.2 ColPack.0.0 ColGain.0.1.3 ColGain.2.0.0 ColGain.2.0.1 ColGain.2.0.2 ColGain.2.0.3 ColQ.0.0
MapQ.0.0 ColGain.2.1.0 MapQ.1.0 MapQ.0.1 ColQ.0.1 RowQ.2 ColGain.2.1.1 ColGain.2.1.2 MapQ.1.1 ColGain.2.1.3
OutCopy.0.0 OutCopy.0.1 OutCopy.1.0 OutCopy.1.1 OutCopy.2.0 RowQ.3 OutCopy.2.1 OutCopy.3.0 OutCopy.3.1
OutCopy.4.0 OutCopy.4.1 ColQ.2.0 OutCopy.5.0 ColQ.2.1 OutCopy.5.1 OutCopy.6.0 OutCopy.6.1 OutCopy.7.0
OutCopy.8.0 OutMin.7.1 OutMin.8.1 OutCopy.9.0 RowQ.6 OutMin.9.1 OutCopy.10.1 OutMin.10.0 OutCopy.11.1
OutMin.11.0 RowQ.7 OutMin.12.0 OutMin.12.1 OutCopy.13.1 OutMin.13.0 OutCopy.14.1 OutMin.14.0 OutCopy.15.1
OutMin.15.0
"""
SCALAR_ORDER = """
Gain GainRow.0 RowGain.4.0 RowGain.4.1 RowGain.5.0 RowGain.5.1 RowGain.6.0 FiltPack.0.1.0 FiltPack.0.1.1
GainRow.2 RowGain.6.1 FiltPack.0.1.2 FiltPack.1.0.0 FiltPack.1.0.1 FiltPack.1.0.2 RowGain.7.0 RowGain.7.1
RowPack.4 FiltPack.1.1.0 FiltPack.1.1.1 FiltPack.1.1.2 RowPack.5 OccPack.2.1 MapPack.0.0.0 MapPack.0.0.1
MapPack.0.0.2 MapPack.0.0.3 MapPack.1.0.0 MapPack.1.0.1 MapPack.1.0.2 MapPack.1.0.3 MapPack.0.1.0 ColPack.0.1
MapPack.0.1.1 MapPack.0.1.2 MapPack.0.1.3 MapPack.1.1.0 MapPack.1.1.1 RowGain.12.0 MapPack.1.1.2 MapPack.1.1.3
ColPack.2.0 RowPack.6 RowPack.7 RowGain.12.1 RowGain.13.0 ColPack.2.1 RowGain.13.1 RowGain.14.0 RowGain.14.1
RowGain.15.0 RowGain.15.1 OutCopy.7.1 OutCopy.8.1 RowPack.12 RowPack.13 RowPack.14 OutCopy.9.1 OutCopy.10.0
RowPack.15 OutCopy.11.0 OutCopy.12.0 OutCopy.12.1 OutCopy.13.0 OutCopy.14.0 OutCopy.15.0
"""


def tile_exponential_shadow_visibility_s12_kernel(
    tc, foot_words, foot_scales, atom_words, atom_scales, filt, occ, recv, out
):
    nc = tc.nc

    with ExitStack() as ctx:
        keep = ctx.enter_context(tc.tile_pool(name="keep", bufs=1))
        work = ctx.enter_context(tc.tile_pool(name="work", bufs=3))
        ring = ctx.enter_context(tc.tile_pool(name="ring", bufs=10))
        psum = ctx.enter_context(tc.psum_pool(name="psum", bufs=8))
        ctx.enter_context(tc.manual_schedule())

        atom_c = keep.tile([P, 2 * TEX], U8, name="atom_c", align_bytes=64)
        atom_s = keep.tile([P, TEX], U8, name="atom_s", align_bytes=64)
        atom_oc = [keep.tile([P, 1024], U8, name=f"atom_oc{g}", align_bytes=64) for g in range(N_GROUPS)]
        atom_os = [keep.tile([P, 512], U8, name=f"atom_os{g}", align_bytes=64) for g in range(N_GROUPS)]
        gain_row = {quad: keep.tile([P, 512], F32, name=f"gain_row{quad}") for quad in COLUMN_QUADS}
        foot_c = keep.tile([P, 2 * REC], U8, name="foot_c", align_bytes=64)
        foot_s = keep.tile([P, REC], U8, name="foot_s", align_bytes=64)
        ident = keep.tile([P, P], F32, name="ident")
        recv16 = keep.tile([P, P], BF16, name="recv16")
        recv32 = keep.tile([P, P], F32, name="recv32")
        gain = keep.tile([P, N_TILES], F32, name="gain")
        exp_seed = keep.tile([P, 1], F32, name="exp_seed")

        def codes_and_scales(name, rows, columns):
            codes = [[keep.tile([P, 512], U32, name=f"{name}_q{r}{c}", align_bytes=64) for c in range(columns)] for r in range(rows)]
            scales = [[keep.tile([P, 512], U8, name=f"{name}_s{r}{c}", align_bytes=64) for c in range(columns)] for r in range(rows)]
            return codes, scales

        filt_q, filt_s = codes_and_scales("filt", N_GROUPS, N_CHUNKS)
        occ_q, occ_s = codes_and_scales("occ", N_CHUNKS, 2)
        e_q, e_s = codes_and_scales("e", N_GROUPS, 2)
        f_q = [keep.tile([P, 512], U32, name=f"f_q{k}", align_bytes=64) for k in range(N_TILES // 2)]
        f_s = [keep.tile([P, 512], U8, name=f"f_s{k}", align_bytes=64) for k in range(N_TILES // 2)]
        filt_raw = [[keep.tile([P, 2, RAW], BF16, name=f"filt_raw{g}{jp}") for jp in range(2)] for g in range(N_GROUPS)]
        occ_raw = [[ring.tile([P, 2048], BF16, name=f"occ_raw{c}{h}", tag="ring") for h in range(2)] for c in range(N_CHUNKS)]

        nc.vector.memset(atom_s[:].bitcast(I32), 0)
        nc.vector.memset(foot_s[:].bitcast(I32), 0)
        nc.vector.memset(ident[:], 0.0)
        nc.vector.memset(recv16[:], 0.0)
        nc.vector.memset(exp_seed[:], 0.0)

        def load_filt(g, jp):
            rows = filt[512 * g : 512 * (g + 1), :].rearrange("(m j) k -> m j k", j=4)
            nc.sync.dma_start(out=filt_raw[g][jp][:], in_=rows[:, 2 * jp : 2 * jp + 2, :])

        def load_occ(c, h):
            rows = occ[512 * c : 512 * (c + 1), :].rearrange("(p j) l -> p j l", j=4)
            nc.sync.dma_start(
                out=occ_raw[c][h][:].rearrange("p (j l) -> p j l", j=4), in_=rows[:, :, 512 * h : 512 * (h + 1)]
            )

        def load_scales(engine, plane, scales, quarter):
            engine.dma_start(
                out=plane[32 * quarter : 32 * quarter + 4, :].bitcast(I32),
                in_=scales[0][4 * quarter : 4 * quarter + 4, :].bitcast(I32),
            )

        load_filt(0, 0)
        nc.sync.dma_start(out=atom_c[:].bitcast(I32), in_=atom_words[0].bitcast(I32))
        nc.sync.dma_start(out=foot_c[:].bitcast(I32), in_=foot_words[0].bitcast(I32))
        for quarter in range(4):
            load_scales(nc.scalar, atom_s, atom_scales, quarter)
        load_scales(nc.scalar, foot_s, foot_scales, 0)
        nc.gpsimd.affine_select(
            out=ident[:], in_=ident[:], pattern=[[-1, P]], compare_op=NOT_EQUAL, fill=1.0, base=0, channel_multiplier=1
        )
        nc.gpsimd.dma_start(out=recv16[0:N_TILES, :], in_=recv.rearrange("(c n) -> c n", n=P))
        load_scales(nc.gpsimd, foot_s, foot_scales, 3)
        nc.scalar.activation(exp_seed[:], exp_seed[:], EXP)
        load_filt(0, 1)
        load_scales(nc.sync, foot_s, foot_scales, 1)
        load_scales(nc.sync, foot_s, foot_scales, 2)
        for name, first, second in LATER_LOADS:
            if name == "filt":
                load_filt(first, second)
            else:
                load_occ(first, second)

        nc.vector.tensor_copy(out=recv32[:], in_=recv16[:])

        banks = {}

        def new_bank(step):
            banks[step] = psum.tile([P, BANK], F32, name="bank")
            return banks[step]

        def copy_on(engine, dst, src):
            if engine == "V":
                nc.vector.tensor_copy(out=dst, in_=src)
            else:
                nc.scalar.copy(dst, src)

        def quantize(codes, scales, values):
            nc.vector.quantize_mx(out=codes[:].bitcast(FP8X4), scales=scales[:], in_=values[:])

        def recv_t():
            nc.tensor.transpose(new_bank("recv")[:, 0:P], recv32[:], ident[:])

        def make_gain():
            nc.scalar.activation(gain[:], banks["recv"][:, 0:N_TILES], EXP)

        def gain_t(quad):
            bank = new_bank(("gain", quad))
            for i in range(4):
                tile = 4 * quad + i
                nc.tensor.transpose(bank[:, P * i : P * (i + 1)], gain[:, tile : tile + 1].to_broadcast([P, P]), ident[:])

        def make_gain_row(quad):
            nc.scalar.copy(gain_row[quad][:], banks["gain", quad][:])

        natural = {}
        f_values = {}

        def row_mm(tile, g):
            nc.tensor.matmul_mx(
                out=new_bank(("row", tile, g))[:],
                lhsT=foot_c[:, 256 * tile : 256 * (tile + 1)].bitcast(FP4X4),
                lhsT_scale=foot_s[:, P * tile : P * (tile + 1)],
                rhs=atom_c[:, 1024 * g : 1024 * (g + 1)].bitcast(FP4X4),
                rhs_scale=atom_s[:, 512 * g : 512 * (g + 1)],
                start=True,
                stop=True,
            )

        def row_gain(engine, tile, g):
            if tile not in natural:
                natural[tile] = work.tile([P, TEX], BF16, name="natural", bufs=8)
            dst = natural[tile][:, 512 * g : 512 * (g + 1)].rearrange("p (u b i v) -> p u b i v", u=2, i=4, v=2)
            src = banks["row", tile, g][:].rearrange("p (b u v i) -> p u b i v", u=2, i=4, v=2)
            for u in range(2):
                if engine == "V":
                    nc.vector.tensor_scalar_mul(dst[:, u], src[:, u], gain[:, tile : tile + 1])
                else:
                    nc.scalar.activation(dst[:, u], src[:, u], COPY, scale=gain[:, tile : tile + 1])

        def row_t(tile):
            words = natural[tile][:].bitcast(F32)
            bank = new_bank(("row_t", tile))
            for b in range(4):
                nc.tensor.transpose(bank[:, P * b : P * (b + 1)], words[:, P * b : P * (b + 1)], ident[:])

        def row_pack(engine, tile):
            pair, i = divmod(tile, 2)
            if pair not in f_values:
                f_values[pair] = work.tile([P, 2048], BF16, name="f_values", bufs=4, align_bytes=64)
            dst = f_values[pair][:, 1024 * i : 1024 * (i + 1)].bitcast(F32).rearrange("p (g r u) -> p g r u", g=2, u=2)
            copy_on(engine, dst, banks["row_t", tile][:].rearrange("p (g u r) -> p g r u", g=2, u=2))

        def row_q(pair):
            quantize(f_q[pair], f_s[pair], f_values[pair])

        w_gained = {}

        def atom_order(g):
            nc.vector.tensor_copy(
                out=atom_oc[g][:].bitcast(I32).rearrange("p (t b w) -> p t b w", t=4, w=2),
                in_=atom_c[:, 1024 * g : 1024 * (g + 1)].bitcast(I32).rearrange("p (b t w) -> p t b w", t=4, w=2),
            )
            nc.vector.tensor_copy(
                out=atom_os[g][:].bitcast(I32).rearrange("p (t b) -> p t b", t=4),
                in_=atom_s[:, 512 * g : 512 * (g + 1)].bitcast(I32).rearrange("p (b t) -> p t b", t=4),
            )

        def col_mm(quad, g, t):
            nc.tensor.matmul_mx(
                out=new_bank(("col", quad, g, t))[:],
                lhsT=atom_oc[g][:, 256 * t : 256 * (t + 1)].bitcast(FP4X4),
                lhsT_scale=atom_os[g][:, P * t : P * (t + 1)],
                rhs=foot_c[:, 1024 * quad : 1024 * (quad + 1)].bitcast(FP4X4),
                rhs_scale=foot_s[:, 512 * quad : 512 * (quad + 1)],
                start=True,
                stop=True,
            )

        def col_gain(quad, g, t):
            if (quad, g) not in w_gained:
                w_gained[quad, g] = work.tile([P, 4, 512], BF16, name="w_gained", bufs=2)
            nc.vector.tensor_tensor(
                out=w_gained[quad, g][:, t, :], in0=banks["col", quad, g, t][:], in1=gain_row[quad][:], op=MULT
            )

        def interleave(engine, dst, src):
            copy_on(
                engine,
                dst[:].rearrange("p (c i t) -> p c t i", i=4, t=4),
                src.rearrange("p (t c i) -> p c t i", t=4, i=4),
            )

        def col_pack(engine, quad, g):
            f_values[quad, g] = work.tile([P, 2048], BF16, name="f_values", bufs=4, align_bytes=64)
            interleave(engine, f_values[quad, g], w_gained[quad, g][:].rearrange("p t n -> p (t n)"))

        def col_q(quad, g):
            quantize(f_q[2 * quad + g], f_s[2 * quad + g], f_values[quad, g])

        filt_values = {}
        occ_values = {}

        def filt_t(g, jp, c):
            words = filt_raw[g][jp][:].rearrange("p j k -> p (j k)").bitcast(F32)
            bank = new_bank(("filt", g, jp, c))
            for j in range(2):
                for u in range(2):
                    first = (RAW // 2) * j + 256 * c
                    b = 2 * j + u
                    nc.tensor.transpose(bank[:, P * b : P * (b + 1)], words[:, first + u : first + 256 : 2], ident[:])

        def filt_pack(engine, g, jp, c):
            if (g, c) not in filt_values:
                filt_values[g, c] = work.tile([P, 2048], BF16, name="filt_values", bufs=5, align_bytes=64)
            dst = filt_values[g, c][:].bitcast(F32).rearrange("p (t b x) -> p t b x", t=4, x=8)[:, :, :, 4 * jp : 4 * jp + 4]
            copy_on(engine, dst, banks["filt", g, jp, c][:].rearrange("p (x b t) -> p t b x", t=4, x=4))

        def filt_quant(g, c):
            quantize(filt_q[g][c], filt_s[g][c], filt_values[g, c])

        def occ_pack(engine, c, h):
            occ_values[c, h] = work.tile([P, 2048], BF16, name="occ_values", bufs=4, align_bytes=64)
            interleave(engine, occ_values[c, h], occ_raw[c][h][:])

        def occ_quant(c, h):
            quantize(occ_q[c][h], occ_s[c][h], occ_values[c, h])

        e_values = {}

        def map_mm(g, h, i):
            bank = new_bank(("map", g, h, i))
            for t in range(4):
                for c in range(N_CHUNKS):
                    nc.tensor.matmul_mx(
                        out=bank[:, P * t : P * (t + 1)],
                        lhsT=filt_q[g][c][:, P * t : P * (t + 1)].bitcast(FP8X4),
                        lhsT_scale=filt_s[g][c][:, P * t : P * (t + 1)],
                        rhs=occ_q[c][h][:, P * i : P * (i + 1)].bitcast(FP8X4),
                        rhs_scale=occ_s[c][h][:, P * i : P * (i + 1)],
                        start=(c == 0),
                        stop=(c == N_CHUNKS - 1),
                    )

        def map_pack(engine, g, h, i):
            if (g, h) not in e_values:
                e_values[g, h] = work.tile([P, 2048], BF16, name="e_values", bufs=4, align_bytes=64)
            dst = e_values[g, h][:, 512 * i : 512 * (i + 1)].rearrange("p (n t) -> p n t", t=4)
            copy_on(engine, dst, banks["map", g, h, i][:].rearrange("p (t n) -> p n t", t=4))

        def map_quant(g, h):
            quantize(e_q[g][h], e_s[g][h], e_values[g, h])

        out_tiles = {}
        halves_done = {}

        def out_mm(tile, h):
            bank = new_bank(("out", tile, h))
            for g in range(N_GROUPS):
                if tile // 4 in COLUMN_QUADS:
                    k, j = 2 * (tile // 4) + g, tile % 4
                else:
                    k, j = tile // 2, 2 * (tile % 2) + g
                columns = slice(P * j, P * (j + 1))
                nc.tensor.matmul_mx(
                    out=bank[:],
                    lhsT=f_q[k][:, columns].bitcast(FP8X4),
                    lhsT_scale=f_s[k][:, columns],
                    rhs=e_q[g][h][:].bitcast(FP8X4),
                    rhs_scale=e_s[g][h][:],
                    start=(g == 0),
                    stop=(g == N_GROUPS - 1),
                )

        def store(tile, h):
            halves_done[tile] = halves_done.get(tile, 0) + 1
            if tile == LAST_TILE:
                columns = slice(512 * h, 512 * (h + 1))
                nc.sync.dma_start(out=out[P * tile : P * (tile + 1), columns], in_=out_tiles[tile][:, columns])
            elif halves_done[tile] == 2:
                nc.sync.dma_start(out=out[P * tile : P * (tile + 1), :], in_=out_tiles[tile][:])

        def out_copy(engine, tile, h):
            if tile not in out_tiles:
                out_tiles[tile] = ring.tile([P, FRM], F32, name="out_tile", tag="ring")
            dst = out_tiles[tile][:, 512 * h : 512 * (h + 1)]
            if engine == "V":
                nc.vector.tensor_scalar_min(dst, banks["out", tile, h][:], 1.0)
                store(tile, h)
            else:
                nc.scalar.copy(dst, banks["out", tile, h][:])

        def out_min(tile, h):
            dst = out_tiles[tile][:, 512 * h : 512 * (h + 1)]
            nc.vector.tensor_scalar_min(dst, dst, 1.0)
            store(tile, h)

        def f_ready(tile):
            if tile // 4 in COLUMN_QUADS:
                return [("ColQ", tile // 4, g) for g in range(N_GROUPS)]
            return [("RowQ", tile // 2)]

        kinds = {
            "RecvT": (lambda: [], recv_t, False),
            "Gain": (lambda: [("RecvT",)], make_gain, False),
            "GainT": (lambda quad: [("Gain",)], gain_t, False),
            "GainRow": (lambda quad: [("GainT", quad)], make_gain_row, False),
            "RowMM": (lambda tile, g: [], row_mm, False),
            "RowGain": (lambda tile, g: [("Gain",), ("RowMM", tile, g)], row_gain, True),
            "RowT": (lambda tile: [("RowGain", tile, g) for g in range(N_GROUPS)], row_t, False),
            "RowPack": (lambda tile: [("RowT", tile)], row_pack, True),
            "RowQ": (lambda pair: [("RowPack", 2 * pair + i) for i in range(2)], row_q, False),
            "AtomOrder": (lambda g: [], atom_order, False),
            "ColMM": (lambda quad, g, t: [("AtomOrder", g)], col_mm, False),
            "ColGain": (lambda quad, g, t: [("GainRow", quad), ("ColMM", quad, g, t)], col_gain, False),
            "ColPack": (lambda quad, g: [("ColGain", quad, g, t) for t in range(4)], col_pack, True),
            "ColQ": (lambda quad, g: [("ColPack", quad, g)], col_q, False),
            "FiltT": (lambda g, jp, c: [], filt_t, False),
            "FiltPack": (lambda g, jp, c: [("FiltT", g, jp, c)], filt_pack, True),
            "FiltQ": (lambda g, c: [("FiltPack", g, jp, c) for jp in range(2)], filt_quant, False),
            "OccPack": (lambda c, h: [], occ_pack, True),
            "OccQ": (lambda c, h: [("OccPack", c, h)], occ_quant, False),
            "MapMM": (
                lambda g, h, i: [("FiltQ", g, c) for c in range(N_CHUNKS)] + [("OccQ", c, h) for c in range(N_CHUNKS)],
                map_mm,
                False,
            ),
            "MapPack": (lambda g, h, i: [("MapMM", g, h, i)], map_pack, True),
            "MapQ": (lambda g, h: [("MapPack", g, h, i) for i in range(4)], map_quant, False),
            "OutMM": (lambda tile, h: f_ready(tile) + [("MapQ", g, h) for g in range(N_GROUPS)], out_mm, False),
            "OutCopy": (lambda tile, h: [("OutMM", tile, h)], out_copy, True),
            "OutMin": (lambda tile, h: [("OutCopy", tile, h)], out_min, False),
        }

        def parse(table):
            return [(word.split(".")[0],) + tuple([int(n) for n in word.split(".")[1:]]) for word in table.split()]

        waiting = {"T": parse(TENSOR_ORDER), "V": parse(VECTOR_ORDER), "S": parse(SCALAR_ORDER)}
        called = set()
        while any(waiting.values()):
            before = len(called)
            for engine, steps in waiting.items():
                while steps:
                    step = steps[0]
                    needs, function, takes_engine = kinds[step[0]]
                    if not all([need in called for need in needs(*step[1:])]):
                        break
                    if takes_engine:
                        function(engine, *step[1:])
                    else:
                        function(*step[1:])
                    called.add(step)
                    steps.remove(step)
            if len(called) == before:
                raise ValueError("the tables' orders contradict the steps' needs")
